import numpy as np, ml_dtypes
CORES = [48,51,52,55]
N = 4
import mx_ref
BF = ml_dtypes.bfloat16
def entries(a):
    return np.ascontiguousarray(a.T).reshape(-1)
def table(e):
    return np.ascontiguousarray(np.reshape(e, (-1, 16)).T).astype(np.int32)
def cols(t, e):
    v = np.concatenate([t.reshape(128, -1, 4), np.zeros((128, 1, 4), BF)], axis=1)
    return np.ascontiguousarray(v[:, e]).reshape(128, -1)
def cut(t, i, w=512):
    return t[:, w * i:w * i + w]
def pick(q, e):
    c = np.concatenate([q[0].reshape(128, -1, 4), np.zeros((128, 1, 4), np.uint8)], axis=1); s = np.concatenate([q[1], np.ones((16, 1), np.uint8)], axis=1)
    return (np.ascontiguousarray(c[:, e].reshape(128, -1)), np.ascontiguousarray(s[:, e]))
def join(*qs):
    return (np.concatenate([q[0] for q in qs], axis=1), np.concatenate([q[1] for q in qs], axis=1))
def put(q, e, v):
    c, s = q[0].reshape(128, -1, 4).copy(), q[1].copy(); c[:, e] = v[0].reshape(128, -1, 4); s[:, e] = v[1]
    return (c.reshape(128, -1), s)
def pk(c, s):
    return (np.ascontiguousarray(c), mx_ref.live(s))
def emit(q):
    return q[0], q[1]
def decode(q):
    o = []
    for b in range(4):
        e = np.zeros((128, 128, 4), np.float32); e[np.arange(128), np.arange(128), b] = 1
        o.append(mx_ref.matmul(mx_ref.quantize(e.reshape(128, 512).astype(BF)), q))
    return np.stack(o, axis=2).reshape(128, -1)
def f(rng, *shape):
    return mx_ref.flush((rng.standard_normal(shape, dtype=np.float32) * np.exp2(rng.integers(-2, 3, shape[:-1] + (1,)))).astype(BF))
def wide(rng, *shape, cols=0):
    v = rng.standard_normal(shape, dtype=np.float32) * np.exp2(rng.integers(-12, 13, shape)).astype(np.float32)
    if cols: v *= np.repeat(np.exp2(rng.integers(-cols, cols + 1, shape[:-2] + (1, shape[-1] // 4))) * (rng.random(shape[:-2] + (1, shape[-1] // 4)) > 0.0625), 4, axis=-1).astype(np.float32)
    return mx_ref.flush(v.astype(BF))
A, M, CAPP, R, O = 512, 48, 8, 3, 3
def flat(v):
    return np.concatenate([v[r] for r in range(N)], axis=1)
def ranks(v):
    return np.ascontiguousarray(v.reshape(128, N, -1).transpose(1, 0, 2))
def trim(v):
    v = np.asarray(v).astype(np.float32)
    v[np.abs(v) < np.float32(2.0 ** -16)] = 0
    return v.astype(BF)
def lists(rng):
    return np.stack([np.stack([rng.permutation(A)[:4] for i in range(M)], axis=1) for r in range(N)])
def given(rng, d, x, b, own):
    return {"d": d, "x": x, "b": b, "act": np.stack([table(v.reshape(-1)) for v in own]), "w": f(rng, N, 128, 512 * O)}
def setup_inputs(rng):
    d, own = trim(f(rng, N, 128, 4 * A)), lists(rng)
    every, x, b = flat(d), np.zeros((N, 128, 4 * M), np.float32), np.zeros((N, 128, 4 * M), np.float32)
    for r in range(N):
        for s in range(4): x[r] += np.float32(0.25) * cols(every, A * r + own[r, s]).astype(np.float32)
    x = trim(x)
    for r in range(N):
        b[r] = x[r].astype(np.float32)
        for k in range(3):
            g = rng.integers(0, N * A, M)
            if k == 0: g = np.where(rng.random(M) < 0.25, A * r + own[r, rng.integers(0, 4, M), np.arange(M)], g)
            b[r] += np.repeat(0.5 + rng.random(M), 4).astype(np.float32) * cols(every, g).astype(np.float32)
    return given(rng, d, x, trim(b), own)
def setup_inputs_crowd(rng):
    H, small = 6, np.float32(2.0 ** -10)
    rows = rng.permutation(512)[:H * N]
    hot = np.stack([A * q + rng.permutation(A)[:H] for q in range(N)])
    v = (flat(f(rng, N, 128, 4 * A)).astype(np.float32) * np.float32(0.125)).reshape(128, N * A, 4)
    v[rows // 4, :, rows % 4] = 0
    v[rows // 4, hot.reshape(-1), rows % 4] = 64
    x = f(rng, N, 128, 4 * M).astype(np.float32).reshape(N, 128, M, 4)
    x[:, rows // 4, :, rows % 4] = 0
    b, own, rows = x.copy(), np.zeros((N, 4, M), int), rows.reshape(N, H)
    busy = int(rng.integers(0, N))
    for r in range(N):
        flood = busy if r != busy else (busy + 1) % N
        even = int(rng.choice([q for q in range(N) if q != r and q != flood]))
        n = M // 8
        who = np.full(M, flood)
        who[:n] = -1
        who[n:n + CAPP + 2] = r
        who[n + CAPP + 2:n + 2 * CAPP + 2] = even
        who = rng.permutation(who)
        cold = np.setdiff1d(np.arange(A), hot[r] - A * r)
        for i in range(M):
            q, h = r if who[i] < 0 else int(who[i]), int(rng.integers(0, H))
            own[r, :, i] = rng.permutation(cold)[:4]
            if who[i] < 0: own[r, int(rng.integers(0, 4)), i] = hot[r, h] - A * r
            b[r, rows[q, h] // 4, i, rows[q, h] % 4] = 64
            k = rows[(q + int(rng.integers(1, N))) % N, int(rng.integers(0, H))]
            b[r, k // 4, i, k % 4] = 56
    return given(rng, ranks(trim(v * small)), trim((x * small).reshape(N, 128, 4 * M)), trim((b * small).reshape(N, 128, 4 * M)), own)
def setup_inputs_edge(rng):
    k = rng.integers(1, 8, (N * A, 4))
    v = np.zeros((128, N * A, 4))
    v[:64] = 2.0 ** 28
    for j in range(4):
        g = np.sort(rng.permutation(N * A)[:2])
        k[g[0], j], k[g[1], j] = 7, 8
        v[64 + 8 * j, :, 0] = k[:, j] * 2.0 ** 20
    v[96:] = rng.standard_normal((32, N * A, 4)) * 2.0 ** 20
    x = np.zeros((N, 128, M, 4))
    x[:, 96:] = rng.standard_normal((N, 32, M, 4)) * 2.0 ** 20
    b = x.copy()
    for r in range(N):
        u = np.where(rng.permutation(M) < M // 2, 2.0 ** 28, -(2.0 ** 28))
        x[r, :64] = -u[None, :, None]
        b[r, :64] = u[None, :, None]
        b[r, 64 + 8 * rng.integers(0, 4, M), np.arange(M), 0] = 2.0 ** 22
    return given(rng, ranks(trim(v)), trim(x.reshape(N, 128, 4 * M)), trim(b.reshape(N, 128, 4 * M)), lists(rng))
def setup_inputs_ties(rng):
    P = A // 8
    base = rng.standard_normal((128, P, 4))
    base[:, 0] = 0
    of = np.zeros((N, A), int)
    for q in range(N):
        first = np.arange(q, P, N)
        have = np.flatnonzero((np.arange(P) % N <= q) & (np.arange(P) > 0))
        of[q] = rng.permutation(np.concatenate([first, rng.choice(have, A - first.size)]))
    x = trim(rng.standard_normal((N, 128, M, 4)))
    b, own = x.astype(np.float32), lists(rng)
    for r in range(N):
        n = np.bincount(of[r], minlength=P)
        n[0] = 0
        p = int(np.argmax(n))
        spots = np.flatnonzero(of[r] == p)[1:]
        want, o = rng.integers(1, P, M), rng.permutation(M)
        for i in o[:M // 2]:
            want[i] = p
            own[r, :, i] = rng.permutation(spots)[:4]
        want[o[-1]] = 0
        if r == 0: own[0, :, int(o[-1])] = np.concatenate([[0], rng.permutation(np.flatnonzero(of[0] != of[0, 0]))[:3]])
        b[r] += (4 * base[:, want]).astype(np.float32)
    return given(rng, ranks(trim(base[:, of.reshape(-1)])), x.reshape(N, 128, 4 * M), trim(b.reshape(N, 128, 4 * M)), own)
def setup_inputs_spread(rng):
    return given(rng, trim(wide(rng, N, 128, 4 * A, cols=2)), trim(wide(rng, N, 128, 4 * M, cols=2)), trim(wide(rng, N, 128, 4 * M, cols=2)), lists(rng))
def check_inputs(d):
    bad = []
    for k, lo, hi in (("d", -16, 28), ("x", -16, 28), ("b", -16, 28), ("w", -30, 30)):
        v = np.abs(d[k].astype(np.float32))
        if not (np.isfinite(v).all() and ((v == 0) | (v >= 2.0 ** lo) & (v <= 2.0 ** hi)).all()): bad.append("a value of " + k)
    for r in range(N):
        a = entries(d["act"][r])
        if a.min() < 0 or a.max() >= A: bad.append("an entry of act")
        s = np.sort(a.reshape(4, M), axis=0)
        if (s[1:] == s[:-1]).any(): bad.append("two entries of act for one point are equal")
    return bad
def reference(d, x, b, act, w):
    every = mx_ref.quantize(np.ascontiguousarray(flat(d)))
    at, goal = flat(x).astype(np.float32), flat(b).astype(np.float32)
    own = np.stack([entries(act[r]).reshape(4, M).astype(np.int64) + A * r for r in range(N)])
    wq = [[mx_ref.quantize(np.ascontiguousarray(cut(w[r], o))) for o in range(O)] for r in range(N)]
    K = -(-N * M // 128)
    every_point = np.arange(M)
    y = np.zeros((N, 128, R * O * 4 * M), np.float32)
    for t in range(R):
        e = np.concatenate([(goal - at).astype(BF), np.zeros((128, 512 * K - 4 * N * M), BF)], axis=1)
        s = np.concatenate([mx_ref.matmul(mx_ref.quantize(np.ascontiguousarray(cut(e, k))), every) for k in range(K)])
        s = s[:N * M].reshape(N, M, N * A) + np.float32(0)
        far = np.argmax(s, axis=2)
        slot = np.stack([np.argmin(s[r, every_point, own[r]], axis=0) for r in range(N)])
        worst = np.stack([own[r, slot[r], every_point] for r in range(N)])
        go = np.zeros((N, M), bool)
        for r in range(N):
            used = np.zeros(N, int)
            for i in range(M):
                g = int(far[r, i])
                if (own[r, :, i] == g).any():
                    go[r, i] = True
                elif used[g // A] < CAPP:
                    used[g // A] += 1
                    go[r, i] = True
                    own[r, slot[r, i], i] = g
        v = decode(pick(every, np.concatenate([far.reshape(-1), worst.reshape(-1)]))).reshape(128, 2, N * M, 4)
        old = at.reshape(128, N * M, 4)
        new = ((v[:, 0] - v[:, 1]) * np.float32(0.25) + old).astype(BF).astype(np.float32)
        at = np.where(go.reshape(1, -1, 1), new, old).reshape(128, -1)
        for r in range(N):
            q = pick(every, own[r].reshape(-1))
            for o in range(O):
                i = (t * O + o) * 4 * M
                y[r, :, i:i + 4 * M] = mx_ref.matmul(wq[r][o], q)
    oc, osc = np.zeros((N, 128, 16 * M), np.uint8), np.zeros((N, 16, 4 * M), np.uint8)
    for r in range(N): oc[r], osc[r] = emit(pick(every, own[r].reshape(-1)))
    return {"y": y, "px": ranks(at), "oc": oc, "osc": osc, "an": own.astype(np.float32)}

@@ -1,0 +1,621 @@
+import numpy as np
+from concourse.bass import DstId, RemoteDMATransfer
+from concourse.mybir import dt, AluOpType, AxisListType, ActivationFunctionType
+
+A, M, CAPP, R, O = 512, 48, 8, 3, 3
+F32, BF, I32, U16, Q4, U8 = "float32", "bfloat16", "int32", "uint16", "float8_e4m3fn_x4", "uint8"
+PW = 1026
+BIG = 1.0e29
+CUT = 384
+
+SCRATCH = {
+    "xi": ("sbuf", [128, 192], BF), "bi": ("sbuf", [128, 192], BF), "di": ("sbuf", [128, 2048], BF),
+    "wi": ("sbuf", [128, 1536], BF), "ai": ("sbuf", [128, 12], I32), "af": ("sbuf", [128, 12], F32),
+    "zt": ("sbuf", [128, 576], BF), "et": ("sbuf", [128, 512], BF), "ct": ("sbuf", [128, 2064], BF),
+    "pi": ("sbuf", [128, 4], I32), "cc": ("sbuf", [128, 12], F32), "it": ("sbuf", [128, 56], F32),
+    "ip": ("sbuf", [128, 192], F32), "idn": ("sbuf", [128, 256], F32),
+    "tri": ("sbuf", [128, 64], F32), "s4": ("sbuf", [128, 20], F32), "pen": ("sbuf", [128, 192], F32),
+    "psv": ("sbuf", [128, 3 * PW], F32), "phm": ("sbuf", [128, 3 * PW], F32),
+    "jk": ("sbuf", [128, 2240], BF), "ad": ("sbuf", [128, 192], F32), "pa": ("sbuf", [128, 192], F32),
+    "sm": ("sbuf", [128, 144], F32), "num": ("sbuf", [128, 16], F32), "nt": ("sbuf", [128, 64], F32),
+    "sd0": ("sbuf", [128, 24], F32), "sd1": ("sbuf", [128, 24], F32), "so": ("sbuf", [128, 24], F32),
+    "uu": ("sbuf", [128, 96], F32), "kk": ("sbuf", [128, 96], F32), "sam": ("sbuf", [128, 97], F32),
+    "gg": ("sbuf", [128, 144], F32), "rm": ("sbuf", [128, 9], F32),
+    "ofs": ("sbuf", [128, 176], U16),
+    "xp0": ("sbuf", [128, 576], BF), "xp1": ("sbuf", [128, 576], BF), "xp2": ("sbuf", [128, 576], BF),
+    "pxs": ("sbuf", [128, 192], F32), "ys": ("sbuf", [128, 1728], F32),
+    "pss": ("psum", [128, 1024], F32), "psh": ("psum", [128, 1024], F32), "psd": ("psum", [128, 2048], F32),
+}
+for _n, _w in (("h", 1024), ("w", 384), ("k", 1024), ("e", 128), ("m", 48), ("l", 416), ("c", 288), ("f", 272),
+               ("ew0", 352), ("ew1", 352), ("ew2", 224), ("win0", 432), ("win1", 432), ("win2", 432), ("win3", 192)):
+    SCRATCH[_n + "q"] = ("sbuf", [128, _w], Q4)
+    SCRATCH[_n + "s"] = ("sbuf", [128, _w], U8)
+
+NDMA = 20
+SEMAPHORES = (["cv", "cs", "cp", "cg", "sent", "ah0", "ah1"] + ["ae%d" % t for t in range(R)]
+              + ["am%d" % t for t in range(R)] + ["ac%d" % t for t in range(R)] + ["dm%d" % i for i in range(NDMA)])
+ENG = {"v": "cv", "s": "cs", "p": "cp", "g": "cg"}
+CYC, WAKE, CALL, ROW, RATE = 1.0, 60.0, 350.0, 2.0, 250.0
+LAG = {"remote": 1500.0, "dma": 2000.0}
+COSTS = ((0.85, 30.0, 200.0, 1200.0), (1.0, 60.0, 350.0, 1500.0), (1.1, 120.0, 500.0, 2200.0))
+TRIES = 1200
+
+
+def V(name, c0, c1, step=1, p0=0, p1=128):
+    return (name, c0, c1, step, p0, p1)
+
+
+def col(name, c):
+    return (name, c, c + 1, 1, 0, 128)
+
+
+def quad(v, q):
+    return (v[0], v[1], v[2], v[3], 32 * q, 32 * q + 32)
+
+
+def width(v):
+    return len(range(v[1], v[2], v[3]))
+
+
+def depend(ops):
+    lastw, lastr, out = {}, {}, []
+
+    def cells(v):
+        name, c0, c1, step, p0, p1 = v
+        if SCRATCH[name][0] == "psum":
+            return (slice(0, 128), slice(c0 // 512 * 512, -(-c1 // 512) * 512))
+        return (slice(p0, p1), slice(c0, c1, step))
+
+    for i, (q, kind, fn, reads, writes, extra, busy, late) in enumerate(ops):
+        deps, order = set(), set()
+        for v in list(reads) + list(writes):
+            if v[0] not in lastw:
+                lastw[v[0]] = np.full(SCRATCH[v[0]][1], -1, np.int32)
+                lastr[v[0]] = []
+        for v in reads:
+            deps.update(np.unique(lastw[v[0]][cells(v)]).tolist())
+        for v in list(writes) + [v for v in reads if SCRATCH[v[0]][0] == "psum"]:
+            for j, a in lastr[v[0]]:
+                if a[cells(v)].any() and (v in writes or ops[j][0] != q):
+                    deps.add(j)
+        for v in writes:
+            for j in np.unique(lastw[v[0]][cells(v)]).tolist():
+                (order if j >= 0 and q == "p" and ops[j][0] == "p" else deps).add(j)
+        deps.discard(-1)
+        deps.discard(i)
+        if kind == "ext":
+            order.update(extra[2])
+        if kind == "dma":
+            order.update(extra)
+        out.append((deps, order))
+        for v in writes:
+            lastw[v[0]][cells(v)] = i
+            for j, a in lastr[v[0]]:
+                a[cells(v)] = False
+            lastr[v[0]] = [(j, a) for j, a in lastr[v[0]] if a.any()]
+        for v in reads:
+            a = np.zeros(SCRATCH[v[0]][1], bool)
+            a[cells(v)] = True
+            lastr[v[0]].append((i, a))
+    return out
+
+
+def landed(op, issued, lag, free):
+    if not lag:
+        return issued
+    free["dma"] = max(issued + 0.6 * lag, free.get("dma", 0.0)) + op[7]
+    return free["dma"] + 0.4 * lag
+
+
+def listed(ops, dep, nudge):
+    n = len(ops)
+    pred = [sorted(d | o) for d, o in dep]
+    succ = [[] for _ in ops]
+    for i in range(n):
+        for j in pred[i]:
+            succ[j].append(i)
+    level = [0.0] * n
+    for i in range(n - 1, -1, -1):
+        level[i] = ops[i][6] + ops[i][7] + LAG.get(ops[i][1], 0.0) + max([level[k] + WAKE for k in succ[i]] + [0.0])
+    level = [a + b for a, b in zip(level, nudge)]
+    left = [len(p) for p in pred]
+    ready = {i: 0.0 for i in range(n) if not left[i]}
+    done, begun, free, order = [0.0] * n, [0.0] * n, {}, []
+    while ready:
+        x = min(ready, key=lambda i: (max(ready[i], free.get(ops[i][0], 0.0)), -level[i], i))
+        q = ops[x][0]
+        now = max(ready[x], free.get(q, 0.0))
+        near = [i for i in ready if ops[i][0] == q and ready[i] < now + ops[x][6] and level[i] > level[x] + ops[x][6] + 200.0]
+        if near:
+            x = max(near, key=lambda i: level[i])
+            now = max(now, ready[x])
+        del ready[x]
+        order.append(x)
+        if q != "x":
+            free[q] = now + ops[x][6]
+        begun[x], done[x] = now, landed(ops[x], now + ops[x][6], LAG.get(ops[x][1], 0.0), free)
+        for k in succ[x]:
+            left[k] -= 1
+            if not left[k]:
+                ready[k] = max(done[j] + WAKE if j in dep[k][0] else (done[j] if ops[k][1] == "ext" else begun[j]) for j in pred[k])
+    return order
+
+
+def span(ops, dep, order, slow, wake, call, flight):
+    free, done, begun = {}, {}, {}
+    for i in order:
+        q, kind, busy = ops[i][0], ops[i][1], ops[i][6]
+        if kind == "op":
+            busy *= slow
+        elif kind == "remote":
+            busy = call
+        s = free.get(q, 0.0) if q != "x" else 0.0
+        for j in dep[i][0]:
+            s = max(s, done[j] + wake)
+        for j in dep[i][1]:
+            s = max(s, done[j] if kind == "ext" else begun[j])
+        begun[i], free[q] = s, s + busy
+        done[i] = landed(ops[i], s + busy, flight if kind == "remote" else LAG.get(kind, 0.0), free)
+    return max(done.values())
+
+
+def schedule(ops, dep):
+    rng = np.random.RandomState(1)
+    best = None
+    for k in range(TRIES):
+        nudge = np.zeros(len(ops)) if best is None else best[2] + rng.normal(0.0, 400.0, len(ops)) * (rng.random_sample(len(ops)) < 0.04)
+        order = listed(ops, dep, nudge.tolist())
+        cost = sum(span(ops, dep, order, *c) / (c[0] * 3.0 + c[3] / 1000.0) for c in COSTS)
+        if best is None or cost < best[0]:
+            best = (cost, order, nudge)
+    return best[1]
+
+
+def emit(g, T, ops):
+    queues = {"v": g.vector, "s": g.scalar, "p": g.tensor, "g": g, "y": g.sync}
+    dep = depend(ops)
+    count, known, token, seen, total, place = {}, {k: {} for k in queues}, {}, {}, {}, {}
+    ndma = 0
+    for i in schedule(ops, dep):
+        q, kind, fn, reads, writes, extra = ops[i][:6]
+        place[i] = len(place)
+        if kind == "ext":
+            token[i], seen[i] = extra[:2], {}
+            total[extra[0]] = extra[1]
+            continue
+        kn = known[q]
+        for j in sorted(dep[i][0], key=lambda j: -place[j]):
+            s, n = token[j]
+            if kn.get(s, 0) < n:
+                queues[q].wait_ge(T.sem[s], n)
+                kn[s] = n
+                for s2, n2 in seen[j].items():
+                    kn[s2] = max(kn.get(s2, 0), n2)
+        seen[i] = dict(kn)
+        if kind == "remote":
+            fn()
+            total["sent"] = total.get("sent", 0) + extra
+        elif kind == "dma":
+            s = "dm%d" % ndma
+            ndma += 1
+            fn(queues[q]).then_inc(T.sem[s], 16)
+            total[s] = 16
+            token[i] = (s, 16)
+        else:
+            s = ENG[q]
+            count[s] = count.get(s, 0) + 1
+            fn().then_inc(T.sem[s], 1)
+            total[s] = count[s]
+            token[i] = (s, count[s])
+    for s, n in total.items():
+        g.wait_ge(T.sem[s], n)
+
+
+def rank_program(g, core, T, topo):
+    rank = T.rank_of(core)
+    if rank is None:
+        return
+    cores = list(T.cores)
+    mine = [r for r in range(len(cores)) if topo.die(cores[r]) == topo.die(core)]
+    other = [r for r in range(len(cores)) if r not in mine]
+    assert len(mine) == 2 and len(other) == 2 and mine[1] == mine[0] + 1 and other[1] == other[0] + 1
+    me = mine.index(rank)
+    mate, peer = cores[mine[1 - me]], cores[other[me]]
+    base_l, base_r = mine[0] * A, other[0] * A
+    ops = []
+    alu, act = AluOpType, ActivationFunctionType
+
+    def ap(v):
+        name, c0, c1, step, p0, p1 = v
+        return T[name][p0:p1, c0:c1] if step == 1 else T[name][p0:p1, c0:c1:step]
+
+    def sc(x):
+        return ap(x) if isinstance(x, tuple) else x
+
+    def views(*xs):
+        return [x for x in xs if isinstance(x, tuple)]
+
+    def add(q, fn, reads, writes, cycles, kind="op", extra=None, late=0.0):
+        ops.append((q, kind, fn, reads, writes, extra, max(cycles, 64) * CYC if kind == "op" else cycles, late))
+        return len(ops) - 1
+
+    def ts(out, in0, s1, op0, s2=None, op1=None):
+        if op1 is None:
+            add("v", lambda: g.vector.tensor_scalar(ap(out), ap(in0), sc(s1), None, op0), views(in0, s1), [out], width(out))
+        else:
+            add("v", lambda: g.vector.tensor_scalar(ap(out), ap(in0), sc(s1), sc(s2), op0, op1), views(in0, s1, s2), [out], width(out))
+
+    def tt(out, in0, in1, op):
+        add("v", lambda: g.vector.tensor_tensor(ap(out), ap(in0), ap(in1), op), [in0, in1], [out],
+            width(out) * (1 if SCRATCH[in0[0]][0] == "psum" else 2))
+
+    def cp(out, in_):
+        add("v", lambda: g.vector.tensor_copy(ap(out), ap(in_)), [in_], [out], width(out))
+
+    def ms(out, c):
+        add("v", lambda: g.vector.memset(ap(out), c), [], [out], width(out) // (2 if SCRATCH[out[0]][2] == BF else 1))
+
+    def red(out, in_, op):
+        add("v", lambda: g.vector.tensor_reduce(ap(out), ap(in_), AxisListType.X, op), [in_], [out], width(in_))
+
+    def scan(out, d0, d1, init, op0, op1):
+        add("v", lambda: g.vector.tensor_tensor_scan(ap(out), ap(d0), ap(d1), sc(init), op0, op1), views(d0, d1, init), [out], width(out))
+
+    def tr(out, in_):
+        add("v", lambda: g.vector.transpose(ap(out), ap(in_)), [in_], [out], width(out))
+
+    def pair(name, c0, c1):
+        return V(name + "q", c0, c1), V(name + "s", c0, c1)
+
+    def quant(name, c0, c1, in_):
+        q, s = pair(name, c0, c1)
+        add("v", lambda: g.vector.quantize_mx(ap(q), ap(s), ap(in_)), [in_], [q, s], 15 + width(in_) * 0.27)
+
+    def mm(out, lhs, rhs, start=True, stop=True):
+        (lq, ls), (rq, rs) = lhs, rhs
+        add("p", lambda: g.tensor.matmul_mx(ap(out), ap(lq), ap(ls), ap(rq), ap(rs), start, stop), [lq, ls, rq, rs], [out],
+            (width(out) + 16) * 0.6)
+
+    def pick(out, win, off):
+        add("s", lambda: g.scalar.activation(ap(out[1]), ap(win[1]).indirect(ap(off)), act.Copy), [win[1], off], [out[1]],
+            80 + 1.5 * width(out[1]))
+        add("v", lambda: g.vector.tensor_copy(ap(out[0]).bitcast(dt.uint32), ap(win[0]).bitcast(dt.uint32).indirect(ap(off))),
+            [win[0], off], [out[0]], 60 + 1.5 * width(out[0]))
+
+    def sgather(out, win, off):
+        add("s", lambda: g.scalar.activation(ap(out), ap(win).indirect(ap(off)), act.Copy), [win, off], [out], 80 + 1.5 * width(out))
+
+    def scopy(out, in_, scale=None):
+        if scale is None:
+            add("s", lambda: g.scalar.activation(ap(out), ap(in_), act.Copy), [in_], [out], width(out))
+        else:
+            add("s", lambda: g.scalar.activation(ap(out), ap(in_), act.Copy, scale=ap(scale)), [in_, scale], [out], width(out))
+
+    def lin(out, in_, scale=1.0, bias=0.0):
+        add("s", lambda: g.scalar.activation(ap(out), ap(in_), act.Identity, bias=sc(bias), scale=sc(scale)),
+            views(in_, scale, bias), [out], width(out))
+
+    def side(out, in_):
+        add("s", lambda: g.scalar.activation(ap(out), ap(in_), act.Sign, bias=ap(EDGE)), [in_, EDGE], [out], 1)
+
+    def count(junk, in_, last, out, scale=-1.0):
+        add("s", lambda: g.scalar.activation(ap(junk), ap(in_), act.Sign, bias=ap(last), scale=sc(scale), accum_out=ap(out)),
+            views(in_, last, scale), [junk, out], width(in_) + 25)
+
+    def iota(out, pattern, cm=0):
+        if SCRATCH[out[0]][2] == I32:
+            add("g", lambda: g.iota(ap(out), pattern, 0, cm), [], [out], 160 + 2 * width(out))
+        else:
+            add("g", lambda: g.iota(ap(out), pattern, 0, cm, allow_small_or_imprecise_dtypes=True), [], [out], 160 + 2 * width(out))
+
+    def raw(v):
+        return ap(v).bitcast(dt.uint8) if SCRATCH[v[0]][2] == Q4 else ap(v)
+
+    def moved(v):
+        return (v[5] - v[4]) * (ROW + width(v) * {F32: 4, I32: 4, Q4: 4, BF: 2, U16: 2, U8: 1}[SCRATCH[v[0]][2]] / RATE)
+
+    def load(q, out, src, after=(), behind=()):
+        return add(q, lambda e: e.dma_start(ap(out), src), list(after), [out], 100.0, "dma", list(behind), moved(out))
+
+    def store(q, dst, in_, after=()):
+        add(q, lambda e: e.dma_start(dst, raw(in_)), [in_] + list(after), [], 100.0, "dma", [], moved(in_))
+
+    def send(dst, moves, sem):
+        rid, pid = topo.addr(dst)[:2]
+        eng = topo.engines(core, dst)
+        late = sum(moved(i) for o, i in moves)
+        if len(moves) == 1:
+            (out, in_), mask = moves[0], topo.mask(core, dst)
+            return add("g", lambda: g.remote_dma(raw(out), raw(in_), T.sem[sem], T.sem.sent, pid, rid, mask), [in_], [], CALL,
+                       "remote", len(eng), late)
+        k = len(eng) // len(moves)
+        masks = [sum(1 << e for e in eng[k * i:k * i + k]) for i in range(len(moves))]
+        return add("g", lambda: g.remote_dma_fused(
+            [RemoteDMATransfer(dst_ids=[DstId(rid=rid, pnc=pid)], dma_engine_mask=m, remote_sem=T.sem[sem], src=raw(i), dst=raw(o))
+             for m, (o, i) in zip(masks, moves)], local_sem=T.sem.sent), [i for o, i in moves], [], CALL, "remote", len(eng), late)
+
+    def arrive(src, outs, sem, calls):
+        add("x", None, [], outs, 0.0, "ext", (sem, len(calls) * len(topo.engines(src, core)), calls))
+
+    def spread(off):
+        for q in (1, 2, 3):
+            cp(quad(off, q), quad(off, 0))
+
+    def sspread(v):
+        lin(quad(v, 1), quad(v, 0))
+        lin(v[:4] + (64, 128), v[:4] + (0, 64))
+
+    J, J192, J144, BASE, STAY, UNIQ = col("cc", 0), col("cc", 1), col("cc", 2), col("cc", 3), V("cc", 4, 6), col("cc", 6)
+    KF, QF, P32, EDGE, FOUR = col("cc", 7), col("cc", 8), col("cc", 9), col("cc", 10), col("cc", 11)
+    TRI, HALF, S4, J15 = V("tri", 0, 32), V("tri", 32, 64), V("s4", 0, 4), V("s4", 4, 19)
+    OE0, FIRST = V("ofs", 144, 150), V("ofs", 152, 164)
+    own0 = me * A
+    far0 = A - own0
+    banks = [("psh", 512), ("pss", 0), ("pss", 512)]
+
+    def sm(t, i, n=1): return V("sm", 48 * t + i, 48 * t + i + n)
+    def of(t, i, n): return V("ofs", 48 * t + i, 48 * t + i + n)
+    def gg(t, i, n, step=1): return V("gg", 48 * t + i, 48 * t + i + n, step)
+    def osrv(t): return of(t, 0, 3)
+    def oloc(t): return of(t, 4, 3)
+    def oa(t): return of(t, 8, 3)
+    def oe(t): return of(t, 16, 6)
+    def oslot(t): return of(t, 28, 12)
+    def ox(t): return of(t, 40, 3)
+    def num(t): return V("num", 4 * t, 4 * t + 4)
+    def ed(t): return pair("ew%d" % t, 128, 224)
+    def estat(t): return pair("ew%d" % t, 96, 224)
+    def lstat(t): return pair("l", 96 + 96 * t, 224 + 96 * t)
+    def slots(t): return pair("win%d" % t, 0, 192)
+    def xs(t, b, k): return V("xp%d" % t, 144 * b + 48 * k, 144 * b + 48 * k + 48)
+    def pf(buf, t, c0, c1): return V(buf, PW * t + c0, PW * t + c1)
+    def key(t): return col("so", 8 * t + 6)
+    def won(t): return col("sd0", 8 * t + 6)
+    def zz(t): return sm(t, 12)
+
+    def best(ps, buf, stat, t, i, j0):
+        lo, hi, ml, mh = pf(buf, t, 0, 512), pf(buf, t, 512, 1024), pf(buf, t, 511, 512), pf(buf, t, 1023, 1024)
+        pb, cb = pf(buf, t, 1024, 1025), pf(buf, t, 1025, 1026)
+        flip = t == 0 and me == 1
+        for h in ((1, 0) if flip else (0, 1)):
+            mm(V(ps, 512 * h, 512 * h + 512), stat, pair("h", 512 * h, 512 * h + 512))
+        ja, jb = V("jk", j0, j0 + 512), V("jk", j0 + 512, j0 + 1024)
+        if flip:
+            scan(hi, V(ps, 512, 1024), V("zt", 0, 512), -BIG, alu.max, alu.add)
+            count(jb, hi, mh, sm(t, i))
+            ts(sm(t, i + 1), sm(t, i), 512.0, alu.add)
+            scan(lo, V(ps, 0, 512), V("zt", 0, 512), -BIG, alu.max, alu.add)
+            ts(sm(t, i + 2), ml, mh, alu.is_ge, -1.0, alu.mult)
+            ts(sm(t, i + 3), ml, mh, alu.is_ge, ml, alu.mult)
+            count(ja, lo, sm(t, i + 3), cb, sm(t, i + 2))
+            ts(pb, ml, mh, alu.is_lt, sm(t, i + 1), alu.mult)
+            ts(mh, mh, ml, alu.max)
+        else:
+            scan(lo, V(ps, 0, 512), V("zt", 0, 512), -BIG, alu.max, alu.add)
+            count(ja, lo, ml, sm(t, i))
+            scan(hi, V(ps, 512, 1024), V("zt", 0, 512), ml, alu.max, alu.add)
+            count(jb, hi, mh, cb)
+            ts(sm(t, i + 1), ml, mh, alu.is_lt, 512.0, alu.mult)
+            ts(pb, sm(t, i + 1), sm(t, i), alu.max)
+
+    def send_e(t, land, src):
+        calls = [send(peer, [(land[k], src[k])], "ae%d" % t) for k in (0, 1)]
+        arrive(peer, list(land), "ae%d" % t, calls)
+
+    def serve(t):
+        best("pss", "psv", lstat(t), t, 32, 0)
+        note = V("rm", 3 * t, 3 * t + 3)
+        arrive(peer, [note], "am%d" % t, [send(peer, [(note, pf("psv", t, 1023, 1026))], "am%d" % t)])
+        for c in range(3):
+            ts(quad(of(t, c, 1), 0), quad(pf("psv", t, 1024, 1025), c + 1), quad(pf("psv", t, 1025, 1026), c + 1), alu.add)
+        spread(osrv(t))
+        c0 = 96 - 48 * t
+        pick(pair("c", c0, c0 + 48), pair("h", 0, 1024), osrv(t))
+        land = [V("win%dq" % t, 240, 288), V("win%ds" % t, 240, 432)]
+        call = send(peer, [(land[0], V("cq", c0, c0 + 48)), (land[1], V("cs", c0, c0 + 192))], "ac%d" % t)
+        arrive(peer, land, "ac%d" % t, [call])
+
+    def worst(t):
+        mm(V("psh", 0, 192), estat(t), slots(t))
+        tt(V("ad", 0, 192), V("psh", 0, 192), V("pen", 0, 192), alu.add)
+        scan(V("pa", 0, 192), V("ad", 0, 192), V("zt", 0, 192), 2 * BIG, alu.min, alu.add)
+        count(V("jk", 2048, 2240), V("pa", 0, 192), col("pa", 191), sm(t, 13))
+        for c in range(3):
+            lin(quad(gg(t, 36 + c, 1), 0), quad(sm(t, 13), c + 1), -1.0)
+        sspread(gg(t, 36, 3))
+        cp(oa(t), gg(t, 36, 3))
+        pick(pair("f", 128 + 48 * t, 176 + 48 * t), slots(t), oa(t))
+        ts(sm(t, 16, 4), S4, sm(t, 13), alu.add, 0.0, alu.is_equal)
+        lin(sm(t, 8), sm(t, 13), 1.0, J192)
+
+    def move(t, k):
+        end = 288 if k == 1 else 240
+        for b in range(4):
+            mm(V("psd", 512 * b, 512 * b + 128), pair("k", 512 + 128 * b, 640 + 128 * b), pair("f", 48 + 48 * t, 176 + 48 * t), True, False)
+        for b in range(4):
+            mm(V("psd", 512 * b, 512 * b + 128), pair("k", 128 * b, 128 * b + 128), pair("win%d" % t, end - 128, end), False, True)
+        for b in range(4):
+            tt(xs(t, b, k), V("psd", 512 * b + 80, 512 * b + 128), xs(t, b, 0), alu.add)
+        if t + 1 < R:
+            for b in range(4):
+                tt(V("et", 192 * (k - 1) + b, 192 * k, 4), V("bi", b, 192, 4), xs(t, b, k), alu.subtract)
+
+    def near(t):
+        best("psh", "phm", estat(t), t, 36, 1024)
+        pb, cb = pf("phm", t, 1024, 1025), pf("phm", t, 1025, 1026)
+        for c in range(3):
+            lin(quad(gg(t, 32 + c, 1), 0), quad(pb, c + 1), 1.0, quad(cb, c + 1))
+        sspread(gg(t, 32, 3))
+        cp(oloc(t), gg(t, 32, 3))
+        pick(pair("win%d" % t, 192, 240), pair("h", 0, 1024), oloc(t))
+        ts(sm(t, 0), pb, cb, alu.add, float(base_l - base_r), alu.add)
+        side(sm(t, 5), pb)
+        lin(sm(t, 6), sm(t, 5), 1.0, FOUR)
+
+    def near_key(t):
+        ts(sm(t, 20, 4), num(t), sm(t, 0), alu.is_equal)
+        red(sm(t, 7), sm(t, 20, 4), alu.max)
+        lin(col("sd1", 8 * t + 6), sm(t, 7), UNIQ, sm(t, 6))
+        lin(col("sd1", 8 * t + 5), col("sd1", 8 * t + 6), -1.0)
+
+    def y_out(t):
+        for o in range(O):
+            mm(V(banks[o][0], banks[o][1], banks[o][1] + 192), pair("w", 128 * o, 128 * o + 128), slots(t + 1))
+        for o in range(O):
+            c = (t * O + o) * 192
+            (cp if t == R - 1 and o == 1 else scopy)(V("ys", c, c + 192), V(banks[o][0], banks[o][1], banks[o][1] + 192))
+        store("y", T.y[:, 576 * t:576 * t + 576], V("ys", 576 * t, 576 * t + 576), [V("rm", 3 * t + 3, 3 * t + 6)] if t + 1 < R else [])
+
+    def decide(t):
+        mr, pb, cb = col("rm", 3 * t), col("rm", 3 * t + 1), col("rm", 3 * t + 2)
+        ts(won(t), mr, pf("phm", t, 1023, 1024), alu.is_gt if base_r > base_l else alu.is_ge)
+        ts(V("sd1", 8 * t, 8 * t + 4), num(t), pb, alu.subtract, cb, alu.is_equal)
+        side(col("sd1", 8 * t + 4), pb)
+        scan(V("so", 8 * t, 8 * t + 7), V("sd0", 8 * t, 8 * t + 7), V("sd1", 8 * t, 8 * t + 7), 0.0, alu.mult, alu.add)
+        scopy(quad(V("uu", 32, 64), 2), quad(HALF, 1), quad(key(t), 1))
+        ts(V("uu", 0, 32), TRI, key(t), alu.mult)
+        scopy(quad(V("uu", 32, 64), 3), quad(HALF, 2), quad(key(t), 2))
+        ts(quad(V("uu", 64, 96), 3), quad(HALF, 1), quad(key(t), 1), alu.mult)
+        tr(V("kk", 0, 96), V("uu", 0, 96))
+        ts(V("sam", 0, 96), V("kk", 0, 96), key(t), alu.is_equal, -1000.0, alu.mult)
+        red(zz(t), V("sam", 0, 97), alu.add)
+        if t + 1 < R:
+            lin(sm(t, 2), won(t), -48.0, J144)
+            for c in range(3):
+                ts(quad(of(t, 16 + 2 * c, 2), 0), quad(STAY, c + 1), quad(zz(t), c + 1), alu.max, quad(sm(t, 2), c + 1), alu.min)
+            spread(oe(t))
+            quant("ew%d" % t, 224, 352, V("et", 0, 512))
+            pick(ed(t + 1), pair("ew%d" % t, 128, 352), oe(t))
+            send_e(t + 1, pair("l", 224 + 96 * t, 320 + 96 * t), ed(t + 1))
+        lin(sm(t, 9), won(t), 48.0, sm(t, 8))
+        ts(sm(t, 10), key(t), float(CAPP), alu.is_lt, sm(t, 9), alu.mult)
+        lin(sm(t, 24, 4), sm(t, 16, 4), sm(t, 10))
+        ts(sm(t, 28), won(t), -48.0, alu.mult, 96.0, alu.add)
+        both = of(t, 28, 15)
+        ts(sm(t, 4), zz(t), 0.0, alu.is_gt)
+        if t + 1 < R:
+            for c in range(3):
+                lin(quad(gg(t, c, 15 - c, 3), 0), quad(sm(t, 24, 5), c + 1), quad(sm(t, 4), c + 1))
+            sspread(gg(t, 0, 15))
+            tt(gg(t, 16, 15), gg(t, 0, 15), J15, alu.add)
+            cp(both, gg(t, 16, 15))
+        else:
+            for c in range(3):
+                ts(quad(gg(t, c, 15 - c, 3), 0), quad(sm(t, 24, 5), c + 1), quad(zz(t), c + 1), alu.min, 0.0, alu.max)
+            tt(quad(gg(t, 16, 15), 0), quad(gg(t, 0, 15), 0), quad(J15, 0), alu.add)
+            for q in range(4):
+                cp(quad(both, q), quad(gg(t, 16, 15), 0))
+        pick(slots(t + 1), pair("win%d" % t, 0, 288), oslot(t))
+        for b in range(4):
+            sgather(xs(t + 1, b, 0) if t + 1 < R else V("pxs", b, 192, 4), V("xp%d" % t, 144 * b, 144 * b + 144), ox(t))
+        ts(sm(t, 11), pb, cb, alu.add, sm(t, 0), alu.subtract)
+        lin(sm(t, 15), sm(t, 11), won(t), sm(t, 0))
+        ts(sm(t, 14), key(t), float(CAPP), alu.is_lt, -1.0, alu.mult)
+        ts(sm(t, 20, 4), num(t), sm(t, 15), alu.subtract, sm(t, 14), alu.mult)
+        tt(sm(t, 40, 4), sm(t, 20, 4), sm(t, 16, 4), alu.mult)
+        lin(sm(t, 44, 4), sm(t, 40, 4), sm(t, 4), 0.0 if t + 1 < R else BASE)
+        if t + 1 < R:
+            tt(num(t + 1), num(t), sm(t, 44, 4), alu.add)
+        else:
+            for c in range(3):
+                tt(quad(V("nt", c, 12, 3), 0), quad(num(t), c + 1), quad(sm(t, 44, 4), c + 1), alu.add)
+
+    small = [load("y", V("xi", 0, 192), T.x[:, :]), load("s", V("bi", 0, 192), T.b[:, :])]
+    first = load("y", V("di", 0, 4 * CUT), T.d[:, 0:4 * CUT], (), small)
+    rest = load("s", V("di", 4 * CUT, 2048), T.d[:, 4 * CUT:2048], (), [first])
+    load("y", V("ai", 0, 12, 1, 0, 16), T.act[:, :], (), [rest])
+    load("s", V("ai", 0, 12, 1, 16, 32), T.act[:, :], (), [rest])
+    iota(col("pi", 0), [[0, 1]], 1)
+    iota(V("it", 0, 6), [[16, 3], [0, 2]])
+    iota(V("it", 8, 40), [[0, 2], [1, 16]])
+    iota(V("it", 40, 44), [[48, 4]])
+    iota(V("it", 44, 56), [[16, 12]])
+    iota(V("ip", 0, 192), [[0, 4], [1, 48]])
+    iota(V("idn", 0, 128), [[-1, 128]], 1)
+    ms(V("zt", 0, 576), 0.0)
+    lin(V("et", 192, 512), V("zt", 0, 320))
+    ts(col("pi", 1), col("pi", 0), 15, alu.bitwise_and)
+    ts(col("pi", 2), col("pi", 0), 5, alu.arith_shift_right)
+    ts(col("pi", 3), col("pi", 0), 31, alu.bitwise_and)
+    for name in ("ew0", "l", "f", "ew1", "ew2"):
+        quant(name, 0, 128, V("zt", 0, 512))
+    quant("c", 144, 288, V("zt", 0, 576))
+    cp(KF, col("pi", 1))
+    ts(QF, col("pi", 2), 16.0, alu.mult, -16.0, alu.add)
+    cp(P32, col("pi", 3))
+    ts(OE0, V("it", 0, 6), KF, alu.add)
+    ts(J, KF, QF, alu.add)
+    for i in range(4):
+        lin(V("ct", 516 * i, 516 * i + 516), V("zt", 0, 516))
+    ts(V("idn", 128, 256), V("idn", 0, 128), 0.0, alu.is_equal)
+    tt(V("et", 0, 192), V("bi", 0, 192), V("xi", 0, 192), alu.subtract)
+    ts(V("pen", 0, 192), V("ip", 0, 192), J, alu.not_equal, BIG, alu.mult)
+    quant("e", 0, 128, V("et", 0, 512))
+    send_e(0, pair("m", 0, 48), pair("e", 0, 48))
+    pick(ed(0), pair("e", 0, 128), OE0)
+    pick(pair("l", 128, 224), pair("m", 0, 48), OE0)
+    for b in range(4):
+        scopy(xs(0, b, 0), V("xi", b, 192, 4))
+    for i in range(4):
+        lo = 516 * i + 2 + i % 2
+        lin(V("ct", lo, lo + 512, 4), V("idn", 128, 256), 0.25 if i < 2 else -0.25)
+    quant("h", own0, own0 + CUT, V("di", 0, 4 * CUT))
+    quant("h", own0 + CUT, own0 + A, V("di", 4 * CUT, 2048))
+    v, u, s = V("hq", own0, own0 + CUT), V("hq", own0 + CUT, own0 + A), V("hs", own0, own0 + A)
+    arrive(mate, [V("hq", far0, far0 + CUT)], "ah0", [send(mate, [(v, v)], "ah0")])
+    arrive(mate, [V("hq", far0 + CUT, far0 + A), V("hs", far0, far0 + A)], "ah1", [send(mate, [(u, u), (s, s)], "ah1")])
+    cp(quad(V("af", 0, 12), 0), quad(V("ai", 0, 12), 0))
+    sspread(V("af", 0, 12))
+    cp(FIRST, V("af", 0, 12))
+    for s in (1, 0):
+        for b in range(4):
+            lo = 516 * (2 * s + b % 2) + 2 + b % 2 - b
+            quant("k", 512 * s + 128 * b, 512 * s + 128 * b + 128, V("ct", lo, lo + 512))
+    pick(slots(0), pair("h", own0, own0 + A), FIRST)
+    lin(quad(num(0), 0), quad(V("zt", 0, 4), 0))
+    for c in range(3):
+        ts(quad(num(0), c + 1), quad(V("af", c, 12, 3), 0), float(rank * A - base_r), alu.add)
+    lin(S4, V("it", 40, 44), 1.0, J)
+    ts(J192, J, 192.0, alu.add)
+    ts(J144, J, 144.0, alu.add)
+    ts(UNIQ, J, 8.0, alu.mult, 16.0, alu.add)
+    ts(STAY, V("it", 0, 2), QF, alu.add, J, alu.add)
+    ts(TRI, V("it", 8, 40), P32, alu.is_gt)
+    ts(HALF, V("it", 8, 40), 15.5, alu.max, P32, alu.is_gt)
+    lin(V("s4", 4, 16), V("it", 44, 56), 1.0, KF)
+    lin(V("s4", 16, 19), V("it", 44, 47), 1.0, KF)
+    ms(BASE, float(base_r))
+    ms(EDGE, 0.5 - A)
+    ms(FOUR, 4.0)
+    ms(V("sd0", 0, 24), 1.0)
+    lin(V("uu", 32, 96), V("zt", 0, 64))
+    ms(col("sam", 96), 1000.0 * CAPP - 500.0)
+    lin(quad(V("nt", 12, 32), 0), quad(V("zt", 0, 20), 0))
+    lin(V("sd0", 0, 24, 8), V("zt", 0, 3))
+    lin(V("sd0", 4, 24, 8), V("zt", 0, 3), 1.0, UNIQ)
+
+    for t in range(R):
+        if t == 0:
+            worst(t)
+        near(t)
+        serve(t)
+        if t == 0:
+            load("y", V("wi", 0, 1536), T.w[:, :], [V("rm", 0, 3)])
+            for o in range(O):
+                quant("w", 128 * o, 128 * o + 128, V("wi", 512 * o, 512 * o + 512))
+        else:
+            worst(t)
+            y_out(t - 1)
+        near_key(t)
+        move(t, 2)
+        move(t, 1)
+        decide(t)
+
+    y_out(R - 1)
+    store("y", T.oc[:, :], slots(R)[0])
+    for k in range(4):
+        store("ys"[k % 2], T.osc[4 * k:4 * k + 4, :], V("win%ds" % R, 0, 192, 1, 32 * k, 32 * k + 4))
+    store("s", T.px[:, :], V("pxs", 0, 192))
+    tr(quad(V("nt", 32, 64), 0), quad(V("nt", 0, 32), 0))
+    store("y", T.an[:, :], V("nt", 32, 48, 1, 0, 12))
+    emit(g, T, ops)

@@ -26,7 +26,7 @@ SCRATCH = {
     "pxs": ("sbuf", [128, 192], F32), "ys": ("sbuf", [128, 1728], F32),
     "pss": ("psum", [128, 1024], F32), "psh": ("psum", [128, 1024], F32), "psd": ("psum", [128, 2048], F32),
 }
-for _n, _w in (("h", 1024), ("w", 384), ("k", 1024), ("e", 128), ("m", 48), ("l", 416), ("c", 288), ("f", 272),
+for _n, _w in (("h", 1024), ("w", 384), ("k", 1024), ("e", 256), ("m", 192), ("l", 416), ("c", 288), ("f", 272),
                ("ew0", 352), ("ew1", 352), ("ew2", 224), ("win0", 432), ("win1", 432), ("win2", 432), ("win3", 192)):
     SCRATCH[_n + "q"] = ("sbuf", [128, _w], Q4)
     SCRATCH[_n + "s"] = ("sbuf", [128, _w], U8)
@@ -35,10 +35,10 @@ NDMA = 20
 SEMAPHORES = (["cv", "cs", "cp", "cg", "sent", "ah0", "ah1"] + ["ae%d" % t for t in range(R)]
               + ["am%d" % t for t in range(R)] + ["ac%d" % t for t in range(R)] + ["dm%d" % i for i in range(NDMA)])
 ENG = {"v": "cv", "s": "cs", "p": "cp", "g": "cg"}
-CYC, WAKE, CALL, ROW, RATE = 1.0, 60.0, 350.0, 2.0, 250.0
+CYC, WAKE, CALL, ROW, RATE = 1.0, 130.0, 350.0, 2.0, 250.0
 LAG = {"remote": 1500.0, "dma": 2000.0}
-COSTS = ((0.85, 30.0, 200.0, 1200.0), (1.0, 60.0, 350.0, 1500.0), (1.1, 120.0, 500.0, 2200.0))
-TRIES = 1200
+COSTS = ((1.0, 150.0, 350.0, 1500.0), (1.04, 100.0, 500.0, 2000.0), (1.0, 200.0, 350.0, 1700.0))
+TRIES = 1500
 
 
 def V(name, c0, c1, step=1, p0=0, p1=128):
@@ -165,7 +165,7 @@ def schedule(ops, dep):
     for k in range(TRIES):
         nudge = np.zeros(len(ops)) if best is None else best[2] + rng.normal(0.0, 400.0, len(ops)) * (rng.random_sample(len(ops)) < 0.04)
         order = listed(ops, dep, nudge.tolist())
-        cost = sum(span(ops, dep, order, *c) / (c[0] * 3.0 + c[3] / 1000.0) for c in COSTS)
+        cost = sum(span(ops, dep, order, *c) for c in COSTS)
         if best is None or cost < best[0]:
             best = (cost, order, nudge)
     return best[1]
@@ -208,7 +208,8 @@ def emit(g, T, ops):
             total[s] = count[s]
             token[i] = (s, count[s])
     for s, n in total.items():
-        g.wait_ge(T.sem[s], n)
+        if known["g"].get(s, 0) < n:
+            g.wait_ge(T.sem[s], n)
 
 
 def rank_program(g, core, T, topo):
@@ -422,8 +423,8 @@ def rank_program(g, core, T, topo):
         count(V("jk", 2048, 2240), V("pa", 0, 192), col("pa", 191), sm(t, 13))
         for c in range(3):
             lin(quad(gg(t, 36 + c, 1), 0), quad(sm(t, 13), c + 1), -1.0)
-        sspread(gg(t, 36, 3))
-        cp(oa(t), gg(t, 36, 3))
+        for q in range(4):
+            cp(quad(oa(t), q), quad(gg(t, 36, 3), 0))
         pick(pair("f", 128 + 48 * t, 176 + 48 * t), slots(t), oa(t))
         ts(sm(t, 16, 4), S4, sm(t, 13), alu.add, 0.0, alu.is_equal)
         lin(sm(t, 8), sm(t, 13), 1.0, J192)
@@ -444,9 +445,8 @@ def rank_program(g, core, T, topo):
         best("psh", "phm", estat(t), t, 36, 1024)
         pb, cb = pf("phm", t, 1024, 1025), pf("phm", t, 1025, 1026)
         for c in range(3):
-            lin(quad(gg(t, 32 + c, 1), 0), quad(pb, c + 1), 1.0, quad(cb, c + 1))
-        sspread(gg(t, 32, 3))
-        cp(oloc(t), gg(t, 32, 3))
+            ts(quad(of(t, 4 + c, 1), 0), quad(pb, c + 1), quad(cb, c + 1), alu.add)
+        spread(oloc(t))
         pick(pair("win%d" % t, 192, 240), pair("h", 0, 1024), oloc(t))
         ts(sm(t, 0), pb, cb, alu.add, float(base_l - base_r), alu.add)
         side(sm(t, 5), pb)
@@ -493,18 +493,11 @@ def rank_program(g, core, T, topo):
         ts(sm(t, 28), won(t), -48.0, alu.mult, 96.0, alu.add)
         both = of(t, 28, 15)
         ts(sm(t, 4), zz(t), 0.0, alu.is_gt)
-        if t + 1 < R:
-            for c in range(3):
-                lin(quad(gg(t, c, 15 - c, 3), 0), quad(sm(t, 24, 5), c + 1), quad(sm(t, 4), c + 1))
-            sspread(gg(t, 0, 15))
-            tt(gg(t, 16, 15), gg(t, 0, 15), J15, alu.add)
-            cp(both, gg(t, 16, 15))
-        else:
-            for c in range(3):
-                ts(quad(gg(t, c, 15 - c, 3), 0), quad(sm(t, 24, 5), c + 1), quad(zz(t), c + 1), alu.min, 0.0, alu.max)
-            tt(quad(gg(t, 16, 15), 0), quad(gg(t, 0, 15), 0), quad(J15, 0), alu.add)
-            for q in range(4):
-                cp(quad(both, q), quad(gg(t, 16, 15), 0))
+        for c in range(3):
+            ts(quad(gg(t, c, 15 - c, 3), 0), quad(sm(t, 24, 5), c + 1), quad(zz(t), c + 1), alu.min, 0.0, alu.max)
+        tt(quad(gg(t, 16, 15), 0), quad(gg(t, 0, 15), 0), quad(J15, 0), alu.add)
+        for q in range(4):
+            cp(quad(both, q), quad(gg(t, 16, 15), 0))
         pick(slots(t + 1), pair("win%d" % t, 0, 288), oslot(t))
         for b in range(4):
             sgather(xs(t + 1, b, 0) if t + 1 < R else V("pxs", b, 192, 4), V("xp%d" % t, 144 * b, 144 * b + 144), ox(t))
@@ -539,6 +532,7 @@ def rank_program(g, core, T, topo):
     ts(col("pi", 3), col("pi", 0), 31, alu.bitwise_and)
     for name in ("ew0", "l", "f", "ew1", "ew2"):
         quant(name, 0, 128, V("zt", 0, 512))
+    quant("e", 128, 256, V("zt", 0, 512))
     quant("c", 144, 288, V("zt", 0, 576))
     cp(KF, col("pi", 1))
     ts(QF, col("pi", 2), 16.0, alu.mult, -16.0, alu.add)
@@ -551,7 +545,8 @@ def rank_program(g, core, T, topo):
     tt(V("et", 0, 192), V("bi", 0, 192), V("xi", 0, 192), alu.subtract)
     ts(V("pen", 0, 192), V("ip", 0, 192), J, alu.not_equal, BIG, alu.mult)
     quant("e", 0, 128, V("et", 0, 512))
-    send_e(0, pair("m", 0, 48), pair("e", 0, 48))
+    land = [V("mq", 0, 48), V("ms", 0, 192)]
+    arrive(peer, land, "ae0", [send(peer, [(land[0], V("eq", 0, 48)), (land[1], V("es", 0, 192))], "ae0")])
     pick(ed(0), pair("e", 0, 128), OE0)
     pick(pair("l", 128, 224), pair("m", 0, 48), OE0)
     for b in range(4):

@@ -35,10 +35,10 @@ NDMA = 20
 SEMAPHORES = (["cv", "cs", "cp", "cg", "sent", "ah0", "ah1"] + ["ae%d" % t for t in range(R)]
               + ["am%d" % t for t in range(R)] + ["ac%d" % t for t in range(R)] + ["dm%d" % i for i in range(NDMA)])
 ENG = {"v": "cv", "s": "cs", "p": "cp", "g": "cg"}
-CYC, WAKE, CALL, ROW, RATE = 1.0, 130.0, 350.0, 2.0, 250.0
-LAG = {"remote": 1500.0, "dma": 2000.0}
-COSTS = ((1.0, 150.0, 350.0, 1500.0), (1.04, 100.0, 500.0, 2000.0), (1.0, 200.0, 350.0, 1700.0))
-TRIES = 1500
+CYC, WAKE, CALL, ROW, RATE, FIXED = 0.9, 170.0, 350.0, 1.5, 350.0, 60.0
+LAG = {"remote": 1200.0, "dma": 1600.0}
+COSTS = ((0.95, 100.0, 300.0, 1000.0, 100.0), (0.95, 200.0, 300.0, 1200.0, 0.0), (1.1, 150.0, 400.0, 1600.0, 60.0))
+TRIES = 2000
 
 
 def V(name, c0, c1, step=1, p0=0, p1=128):
@@ -141,12 +141,12 @@ def listed(ops, dep, nudge):
     return order
 
 
-def span(ops, dep, order, slow, wake, call, flight):
+def span(ops, dep, order, slow, wake, call, flight, fixed):
     free, done, begun = {}, {}, {}
     for i in order:
         q, kind, busy = ops[i][0], ops[i][1], ops[i][6]
         if kind == "op":
-            busy *= slow
+            busy = (busy - FIXED) * slow + fixed if q == "s" else busy * slow
         elif kind == "remote":
             busy = call
         s = free.get(q, 0.0) if q != "x" else 0.0
@@ -237,7 +237,8 @@ def rank_program(g, core, T, topo):
         return [x for x in xs if isinstance(x, tuple)]
 
     def add(q, fn, reads, writes, cycles, kind="op", extra=None, late=0.0):
-        ops.append((q, kind, fn, reads, writes, extra, max(cycles, 64) * CYC if kind == "op" else cycles, late))
+        busy = max(cycles, 64) * CYC + (FIXED if q == "s" else 0.0) if kind == "op" else cycles
+        ops.append((q, kind, fn, reads, writes, extra, busy, late))
         return len(ops) - 1
 
     def ts(out, in0, s1, op0, s2=None, op1=None):
@@ -293,6 +294,8 @@ def rank_program(g, core, T, topo):
             add("s", lambda: g.scalar.activation(ap(out), ap(in_), act.Copy, scale=ap(scale)), [in_, scale], [out], width(out))
 
     def lin(out, in_, scale=1.0, bias=0.0):
+        if out[0] in ("sm", "sd1"):
+            return ts(out, in_, scale, alu.mult, bias, alu.add)
         add("s", lambda: g.scalar.activation(ap(out), ap(in_), act.Identity, bias=sc(bias), scale=sc(scale)),
             views(in_, scale, bias), [out], width(out))
 

@@ -12,7 +12,7 @@ SCRATCH = {
     "xi": ("sbuf", [128, 192], BF), "bi": ("sbuf", [128, 192], BF), "di": ("sbuf", [128, 2048], BF),
     "wi": ("sbuf", [128, 1536], BF), "ai": ("sbuf", [128, 12], I32), "af": ("sbuf", [128, 12], F32),
     "zt": ("sbuf", [128, 576], BF), "et": ("sbuf", [128, 512], BF), "ct": ("sbuf", [128, 2064], BF),
-    "pi": ("sbuf", [128, 4], I32), "cc": ("sbuf", [128, 12], F32), "it": ("sbuf", [128, 56], F32),
+    "pi": ("sbuf", [128, 4], I32), "cc": ("sbuf", [128, 16], F32), "it": ("sbuf", [128, 56], F32),
     "ip": ("sbuf", [128, 192], F32), "idn": ("sbuf", [128, 256], F32),
     "tri": ("sbuf", [128, 64], F32), "s4": ("sbuf", [128, 20], F32), "pen": ("sbuf", [128, 192], F32),
     "psv": ("sbuf", [128, 3 * PW], F32), "phm": ("sbuf", [128, 3 * PW], F32),
@@ -35,10 +35,12 @@ NDMA = 20
 SEMAPHORES = (["cv", "cs", "cp", "cg", "sent", "ah0", "ah1"] + ["ae%d" % t for t in range(R)]
               + ["am%d" % t for t in range(R)] + ["ac%d" % t for t in range(R)] + ["dm%d" % i for i in range(NDMA)])
 ENG = {"v": "cv", "s": "cs", "p": "cp", "g": "cg"}
-CYC, WAKE, CALL, ROW, RATE, FIXED = 0.9, 170.0, 350.0, 1.5, 350.0, 60.0
-LAG = {"remote": 1200.0, "dma": 1600.0}
-COSTS = ((0.95, 100.0, 300.0, 1000.0, 100.0), (0.95, 200.0, 300.0, 1200.0, 0.0), (1.1, 150.0, 400.0, 1600.0, 60.0))
-TRIES = 2000
+CYC, WAKE, CALL, ROW, RATE, FIXED = 0.9, 150.0, 350.0, 1.0, 500.0, 60.0
+LAG = {"remote": 1000.0, "dma": 1500.0}
+COSTS = ((0.92, 60.0, 500.0, 1400.0, 120.0), (1.1, 120.0, 300.0, 800.0, 60.0), (0.92, 180.0, 300.0, 800.0, 60.0),
+         (0.92, 200.0, 300.0, 900.0, 0.0))
+TRIES = 2200
+ONV = (2, 6, 9, 24)
 
 
 def V(name, c0, c1, step=1, p0=0, p1=128):
@@ -51,6 +53,10 @@ def col(name, c):
 
 def quad(v, q):
     return (v[0], v[1], v[2], v[3], 32 * q, 32 * q + 32)
+
+
+def half(v, h):
+    return (v[0], v[1], v[2], v[3], 64 * h, 64 * h + 64)
 
 
 def width(v):
@@ -294,7 +300,7 @@ def rank_program(g, core, T, topo):
             add("s", lambda: g.scalar.activation(ap(out), ap(in_), act.Copy, scale=ap(scale)), [in_, scale], [out], width(out))
 
     def lin(out, in_, scale=1.0, bias=0.0):
-        if out[0] in ("sm", "sd1"):
+        if out[0] == "sd1" or (out[0] == "sm" and out[1] % 48 in ONV):
             return ts(out, in_, scale, alu.mult, bias, alu.add)
         add("s", lambda: g.scalar.activation(ap(out), ap(in_), act.Identity, bias=sc(bias), scale=sc(scale)),
             views(in_, scale, bias), [out], width(out))
@@ -345,12 +351,16 @@ def rank_program(g, core, T, topo):
         for q in (1, 2, 3):
             cp(quad(off, q), quad(off, 0))
 
+    def spread2(off):
+        cp(quad(off, 1), quad(off, 0))
+        cp(half(off, 1), half(off, 0))
+
     def sspread(v):
         lin(quad(v, 1), quad(v, 0))
-        lin(v[:4] + (64, 128), v[:4] + (0, 64))
+        lin(half(v, 1), half(v, 0))
 
     J, J192, J144, BASE, STAY, UNIQ = col("cc", 0), col("cc", 1), col("cc", 2), col("cc", 3), V("cc", 4, 6), col("cc", 6)
-    KF, QF, P32, EDGE, FOUR = col("cc", 7), col("cc", 8), col("cc", 9), col("cc", 10), col("cc", 11)
+    KF, QF, P32, EDGE, FOUR, N96 = col("cc", 7), col("cc", 8), col("cc", 9), col("cc", 10), col("cc", 11), col("cc", 12)
     TRI, HALF, S4, J15 = V("tri", 0, 32), V("tri", 32, 64), V("s4", 0, 4), V("s4", 4, 19)
     OE0, FIRST = V("ofs", 144, 150), V("ofs", 152, 164)
     own0 = me * A
@@ -426,8 +436,9 @@ def rank_program(g, core, T, topo):
         count(V("jk", 2048, 2240), V("pa", 0, 192), col("pa", 191), sm(t, 13))
         for c in range(3):
             lin(quad(gg(t, 36 + c, 1), 0), quad(sm(t, 13), c + 1), -1.0)
-        for q in range(4):
+        for q in range(2):
             cp(quad(oa(t), q), quad(gg(t, 36, 3), 0))
+        cp(half(oa(t), 1), half(oa(t), 0))
         pick(pair("f", 128 + 48 * t, 176 + 48 * t), slots(t), oa(t))
         ts(sm(t, 16, 4), S4, sm(t, 13), alu.add, 0.0, alu.is_equal)
         lin(sm(t, 8), sm(t, 13), 1.0, J192)
@@ -449,7 +460,7 @@ def rank_program(g, core, T, topo):
         pb, cb = pf("phm", t, 1024, 1025), pf("phm", t, 1025, 1026)
         for c in range(3):
             ts(quad(of(t, 4 + c, 1), 0), quad(pb, c + 1), quad(cb, c + 1), alu.add)
-        spread(oloc(t))
+        spread2(oloc(t))
         pick(pair("win%d" % t, 192, 240), pair("h", 0, 1024), oloc(t))
         ts(sm(t, 0), pb, cb, alu.add, float(base_l - base_r), alu.add)
         side(sm(t, 5), pb)
@@ -467,7 +478,12 @@ def rank_program(g, core, T, topo):
         for o in range(O):
             c = (t * O + o) * 192
             (cp if t == R - 1 and o == 1 else scopy)(V("ys", c, c + 192), V(banks[o][0], banks[o][1], banks[o][1] + 192))
-        store("y", T.y[:, 576 * t:576 * t + 576], V("ys", 576 * t, 576 * t + 576), [V("rm", 3 * t + 3, 3 * t + 6)] if t + 1 < R else [])
+        c = 576 * t
+        if t + 1 < R:
+            store("y", T.y[:, c:c + 576], V("ys", c, c + 576), [V("rm", 3 * t + 3, 3 * t + 6)])
+        else:
+            store("y", T.y[:, c:c + 384], V("ys", c, c + 384))
+            store("y", T.y[:, c + 384:c + 576], V("ys", c + 384, c + 576))
 
     def decide(t):
         mr, pb, cb = col("rm", 3 * t), col("rm", 3 * t + 1), col("rm", 3 * t + 2)
@@ -493,14 +509,16 @@ def rank_program(g, core, T, topo):
         lin(sm(t, 9), won(t), 48.0, sm(t, 8))
         ts(sm(t, 10), key(t), float(CAPP), alu.is_lt, sm(t, 9), alu.mult)
         lin(sm(t, 24, 4), sm(t, 16, 4), sm(t, 10))
-        ts(sm(t, 28), won(t), -48.0, alu.mult, 96.0, alu.add)
+        lin(sm(t, 28), won(t), -48.0, N96)
         both = of(t, 28, 15)
         ts(sm(t, 4), zz(t), 0.0, alu.is_gt)
         for c in range(3):
             ts(quad(gg(t, c, 15 - c, 3), 0), quad(sm(t, 24, 5), c + 1), quad(zz(t), c + 1), alu.min, 0.0, alu.max)
         tt(quad(gg(t, 16, 15), 0), quad(gg(t, 0, 15), 0), quad(J15, 0), alu.add)
-        for q in range(4):
+        for q in range(2 if t + 1 < R else 4):
             cp(quad(both, q), quad(gg(t, 16, 15), 0))
+        if t + 1 < R:
+            cp(half(both, 1), half(both, 0))
         pick(slots(t + 1), pair("win%d" % t, 0, 288), oslot(t))
         for b in range(4):
             sgather(xs(t + 1, b, 0) if t + 1 < R else V("pxs", b, 192, 4), V("xp%d" % t, 144 * b, 144 * b + 144), ox(t))
@@ -585,6 +603,7 @@ def rank_program(g, core, T, topo):
     ms(BASE, float(base_r))
     ms(EDGE, 0.5 - A)
     ms(FOUR, 4.0)
+    ms(N96, 96.0)
     ms(V("sd0", 0, 24), 1.0)
     lin(V("uu", 32, 96), V("zt", 0, 64))
     ms(col("sam", 96), 1000.0 * CAPP - 500.0)

@@ -11,22 +11,21 @@ CUT = 384
 SCRATCH = {
     "xi": ("sbuf", [128, 192], BF), "bi": ("sbuf", [128, 192], BF), "di": ("sbuf", [128, 2048], BF),
     "wi": ("sbuf", [128, 1536], BF), "ai": ("sbuf", [128, 12], I32), "af": ("sbuf", [128, 12], F32),
-    "zt": ("sbuf", [128, 576], BF), "et": ("sbuf", [128, 512], BF), "ct": ("sbuf", [128, 2064], BF),
-    "pi": ("sbuf", [128, 4], I32), "cc": ("sbuf", [128, 16], F32), "it": ("sbuf", [128, 56], F32),
+    "zt": ("sbuf", [128, 576], BF), "et": ("sbuf", [128, 512], BF), "ct": ("sbuf", [128, 1032], BF),
+    "pi": ("sbuf", [128, 4], I32), "cc": ("sbuf", [128, 16], F32), "it": ("sbuf", [128, 96], F32),
     "ip": ("sbuf", [128, 192], F32), "idn": ("sbuf", [128, 256], F32),
-    "tri": ("sbuf", [128, 64], F32), "s4": ("sbuf", [128, 20], F32), "pen": ("sbuf", [128, 192], F32),
+    "tri": ("sbuf", [128, 64], F32), "s4": ("sbuf", [128, 40], F32), "pen": ("sbuf", [128, 192], F32),
     "psv": ("sbuf", [128, 3 * PW], F32), "phm": ("sbuf", [128, 3 * PW], F32),
     "jk": ("sbuf", [128, 2240], BF), "ad": ("sbuf", [128, 192], F32), "pa": ("sbuf", [128, 192], F32),
-    "sm": ("sbuf", [128, 144], F32), "num": ("sbuf", [128, 16], F32), "nt": ("sbuf", [128, 64], F32),
-    "sd0": ("sbuf", [128, 24], F32), "sd1": ("sbuf", [128, 24], F32), "so": ("sbuf", [128, 24], F32),
+    "sm": ("sbuf", [128, 144], F32), "nm": ("sbuf", [128, 32], F32), "rr": ("sbuf", [128, 8], F32), "nt": ("sbuf", [128, 64], F32),
+    "sd0": ("sbuf", [128, 16], F32), "sd1": ("sbuf", [128, 48], F32), "so": ("sbuf", [128, 48], F32),
     "uu": ("sbuf", [128, 96], F32), "kk": ("sbuf", [128, 96], F32), "sam": ("sbuf", [128, 97], F32),
-    "gg": ("sbuf", [128, 144], F32), "rm": ("sbuf", [128, 9], F32),
-    "ofs": ("sbuf", [128, 176], U16),
+    "gg": ("sbuf", [128, 192], F32), "ofs": ("sbuf", [128, 176], U16),
     "xp0": ("sbuf", [128, 576], BF), "xp1": ("sbuf", [128, 576], BF), "xp2": ("sbuf", [128, 576], BF),
-    "pxs": ("sbuf", [128, 192], F32), "ys": ("sbuf", [128, 1728], F32),
+    "pxs": ("sbuf", [128, 256], F32), "ys": ("sbuf", [128, 1728], F32),
     "pss": ("psum", [128, 1024], F32), "psh": ("psum", [128, 1024], F32), "psd": ("psum", [128, 2048], F32),
 }
-for _n, _w in (("h", 1024), ("w", 384), ("k", 1024), ("e", 256), ("m", 192), ("l", 416), ("c", 288), ("f", 272),
+for _n, _w in (("h", 1024), ("w", 384), ("e", 256), ("m", 192), ("l", 416), ("c", 400), ("f", 272),
                ("ew0", 352), ("ew1", 352), ("ew2", 224), ("win0", 432), ("win1", 432), ("win2", 432), ("win3", 192)):
     SCRATCH[_n + "q"] = ("sbuf", [128, _w], Q4)
     SCRATCH[_n + "s"] = ("sbuf", [128, _w], U8)
@@ -35,12 +34,12 @@ NDMA = 20
 SEMAPHORES = (["cv", "cs", "cp", "cg", "sent", "ah0", "ah1"] + ["ae%d" % t for t in range(R)]
               + ["am%d" % t for t in range(R)] + ["ac%d" % t for t in range(R)] + ["dm%d" % i for i in range(NDMA)])
 ENG = {"v": "cv", "s": "cs", "p": "cp", "g": "cg"}
-CYC, WAKE, CALL, ROW, RATE, FIXED = 0.9, 150.0, 350.0, 1.0, 500.0, 60.0
-LAG = {"remote": 1000.0, "dma": 1500.0}
-COSTS = ((0.92, 60.0, 500.0, 1400.0, 120.0), (1.1, 120.0, 300.0, 800.0, 60.0), (0.92, 180.0, 300.0, 800.0, 60.0),
-         (0.92, 200.0, 300.0, 900.0, 0.0))
-TRIES = 2200
-ONV = (2, 6, 9, 24)
+CYC, CALL, ROW, RATE, FIXED = 0.9, 350.0, 1.0, 500.0, 60.0
+DIGITS = "0123456789abcdefghijklmnopqrstuvwxyzABCDEFGHIJKLMNOPQRSTUVWXYZ"
+ORDER = (
+    "02000c0K04060I080S0Q0a120e0G160U110W0g19140k1c1g0i0w0O2I0Y0s0M0C1a1k1y1w2o2A1e1E1G1A1K200u1M221C242c1i1s32282e2u1o1m0y0E360q2g1I2q0A1O0o1Q0m2i1u3i2k2m26383m2U2a3k2W1q3o342Y3q303a3s3u3c3w2K1Z3y3C3G3E1X3e3M3I3K2t3g3Q3O442Q46481S4m4u4o3S1U4a2x2N4q3A4s4c3W5D5A5y4i4k4g4e5E5V4w4y5I5N4G5K2G5G4A5Y2C4E4I4O5O4C2E4M3U58524Q2O4K4W542y5Q5a5X4U5c4S5g4Y565S5e5i5k505o5m5q5s5w5u6662646e686a6c606g6i6u6L6q6s6k6Q6w6M6m6S6A6y6C6U6E3Y6I6W6o6G706Y407E74726O78767G7a7c7I7e428i7K7g7m7k8k7o7O7M7Q828o7s7q8r7u807S847y8m7U867x887A7i8g8e8c8a9z9w7W9u8y8u8C9A8s8A7Y928K8w9F9D9G8E9I948I9R8G8S909U9K8M9T8Q8O7C9M8U9c8W989a9O8Y9k969g9Y9ia2a09e9s9q9o9ma8a6a4aa9WaeacamaHaqao2TagaMasaIaiaOauawaQayaKaSaAaCakaUaWbIaYb0bMbAbKb4b2bCb6b8cmbEbacebRbGbcbibkbgcgbSc0bWbObYbmbockbqaEc2btcic4buccbebwdebUdcdac8dxdgdjdmdodkcadyc6dqe7dAcQcqcMdscudCcocybyducUcCcScsdIdGcOdEcAe8d0cYdKcweacWdOefdMdQdScGdUdWd2cEcKd8eAd4eIekcIeCedeieGeEemerd6epewete2egdYeue5e0eyeMeOeK",
+    "02000K0c04060I080S0M14130e0k0G160Q0P180u0U1a0w1c0s100a0Y1g1y0g0A1k2B1w1Y1A0W1e1U1E1G1K202o1W1C222M1M242c1i281o322e1s2s1m0o2u0i2g362C0q1I0y1O1Q2i1u3q2k2m26383u2U2a3s2W2I3w343A1S2w3y3C3E3I3c3G3K3M2q3g3e3W3O3U3S3i3a2Y0m0C403k423Y301q3m44464C4E4m4L4k484o3o2K4I3Q4G4q0E2G4c5Q5O2Q5T4s6a5U4y4A4u625Y5W6d604Q2O4w4M2E4O2y646e4W4a4Y4U664S6g5054565o525i685m5c5k585s5e5q5a5w6i5u5g5A5y6k5C6m5E5I5G5K5M6o6s6q6u6G6K6I6w6y6M6A766O6Q4g6C786S7a6Y6W6U7c7U6E7W7e7g70727i7Y7k74807o7m8k8i8g4i7q7s8m867u8o4e8y8u7w7C7A7E82847I7K887G8w8q7O8A9i7N8a9e8s8I8d8E7Q8H8C8K8S7y8M8Q9O8e9K9k9M8U908O8Wa79g9Q989T9U9Y9W922Sa98Ya094967Sa29a9c9q9oa49s9m9y9wag9Aaeai9u9G9I9E9CakamaoaqaaauasacaXawb2aEaCaGayb4aIb6aMaKb8aOaAbaaRbcbebgaYbibkaSbmb0bocCbQc2bqcucwbYbSc0bsc8bybAbwc4bUcAbEbGcybCbWbKc6bJccbMbuducadqdscecgdNdwcidFdCdAdPdyckdQdGcqcscmdIbOdSaUd4cEcGdKcKcodUdWdYcSeocOcIcQe0dcemd8cMd6e8e4dge2dee6cWd2eaeccUdkdmdoeQcYeYeAeSeUdaeWeyeCeHdieEd0eMeIeheieKeqeleOefexeuesf0f2f4",
+)
 
 
 def V(name, c0, c1, step=1, p0=0, p1=128):
@@ -72,7 +71,7 @@ def depend(ops):
             return (slice(0, 128), slice(c0 // 512 * 512, -(-c1 // 512) * 512))
         return (slice(p0, p1), slice(c0, c1, step))
 
-    for i, (q, kind, fn, reads, writes, extra, busy, late) in enumerate(ops):
+    for i, (q, kind, fn, reads, writes, extra, busy, late, alt) in enumerate(ops):
         deps, order = set(), set()
         for v in list(reads) + list(writes):
             if v[0] not in lastw:
@@ -82,7 +81,7 @@ def depend(ops):
             deps.update(np.unique(lastw[v[0]][cells(v)]).tolist())
         for v in list(writes) + [v for v in reads if SCRATCH[v[0]][0] == "psum"]:
             for j, a in lastr[v[0]]:
-                if a[cells(v)].any() and (v in writes or ops[j][0] != q):
+                if a[cells(v)].any() and (v in writes or ops[j][0] != q or alt or ops[j][8]):
                     deps.add(j)
         for v in writes:
             for j in np.unique(lastw[v[0]][cells(v)]).tolist():
@@ -106,84 +105,20 @@ def depend(ops):
     return out
 
 
-def landed(op, issued, lag, free):
-    if not lag:
-        return issued
-    free["dma"] = max(issued + 0.6 * lag, free.get("dma", 0.0)) + op[7]
-    return free["dma"] + 0.4 * lag
-
-
-def listed(ops, dep, nudge):
-    n = len(ops)
-    pred = [sorted(d | o) for d, o in dep]
-    succ = [[] for _ in ops]
-    for i in range(n):
-        for j in pred[i]:
-            succ[j].append(i)
-    level = [0.0] * n
-    for i in range(n - 1, -1, -1):
-        level[i] = ops[i][6] + ops[i][7] + LAG.get(ops[i][1], 0.0) + max([level[k] + WAKE for k in succ[i]] + [0.0])
-    level = [a + b for a, b in zip(level, nudge)]
-    left = [len(p) for p in pred]
-    ready = {i: 0.0 for i in range(n) if not left[i]}
-    done, begun, free, order = [0.0] * n, [0.0] * n, {}, []
-    while ready:
-        x = min(ready, key=lambda i: (max(ready[i], free.get(ops[i][0], 0.0)), -level[i], i))
-        q = ops[x][0]
-        now = max(ready[x], free.get(q, 0.0))
-        near = [i for i in ready if ops[i][0] == q and ready[i] < now + ops[x][6] and level[i] > level[x] + ops[x][6] + 200.0]
-        if near:
-            x = max(near, key=lambda i: level[i])
-            now = max(now, ready[x])
-        del ready[x]
-        order.append(x)
-        if q != "x":
-            free[q] = now + ops[x][6]
-        begun[x], done[x] = now, landed(ops[x], now + ops[x][6], LAG.get(ops[x][1], 0.0), free)
-        for k in succ[x]:
-            left[k] -= 1
-            if not left[k]:
-                ready[k] = max(done[j] + WAKE if j in dep[k][0] else (done[j] if ops[k][1] == "ext" else begun[j]) for j in pred[k])
-    return order
-
-
-def span(ops, dep, order, slow, wake, call, flight, fixed):
-    free, done, begun = {}, {}, {}
-    for i in order:
-        q, kind, busy = ops[i][0], ops[i][1], ops[i][6]
-        if kind == "op":
-            busy = (busy - FIXED) * slow + fixed if q == "s" else busy * slow
-        elif kind == "remote":
-            busy = call
-        s = free.get(q, 0.0) if q != "x" else 0.0
-        for j in dep[i][0]:
-            s = max(s, done[j] + wake)
-        for j in dep[i][1]:
-            s = max(s, done[j] if kind == "ext" else begun[j])
-        begun[i], free[q] = s, s + busy
-        done[i] = landed(ops[i], s + busy, flight if kind == "remote" else LAG.get(kind, 0.0), free)
-    return max(done.values())
-
-
-def schedule(ops, dep):
-    rng = np.random.RandomState(1)
-    best = None
-    for k in range(TRIES):
-        nudge = np.zeros(len(ops)) if best is None else best[2] + rng.normal(0.0, 400.0, len(ops)) * (rng.random_sample(len(ops)) < 0.04)
-        order = listed(ops, dep, nudge.tolist())
-        cost = sum(span(ops, dep, order, *c) for c in COSTS)
-        if best is None or cost < best[0]:
-            best = (cost, order, nudge)
-    return best[1]
-
-
-def emit(g, T, ops):
+def emit(g, T, ops, me):
     queues = {"v": g.vector, "s": g.scalar, "p": g.tensor, "g": g, "y": g.sync}
     dep = depend(ops)
+    text = ORDER[me]
+    plan = [divmod(62 * DIGITS.index(text[k]) + DIGITS.index(text[k + 1]), 2) for k in range(0, len(text), 2)]
+    plan = plan or [(i, 0) for i in range(len(ops))]
+    assert sorted(i for i, w in plan) == list(range(len(ops)))
     count, known, token, seen, total, place = {}, {k: {} for k in queues}, {}, {}, {}, {}
     ndma = 0
-    for i in schedule(ops, dep):
+    for i, other in plan:
         q, kind, fn, reads, writes, extra = ops[i][:6]
+        if other:
+            q, fn = ops[i][8][:2]
+        assert all(j in place for j in dep[i][0] | dep[i][1])
         place[i] = len(place)
         if kind == "ext":
             token[i], seen[i] = extra[:2], {}
@@ -229,6 +164,7 @@ def rank_program(g, core, T, topo):
     me = mine.index(rank)
     mate, peer = cores[mine[1 - me]], cores[other[me]]
     base_l, base_r = mine[0] * A, other[0] * A
+    shift = float(base_l - base_r)
     ops = []
     alu, act = AluOpType, ActivationFunctionType
 
@@ -244,8 +180,15 @@ def rank_program(g, core, T, topo):
 
     def add(q, fn, reads, writes, cycles, kind="op", extra=None, late=0.0):
         busy = max(cycles, 64) * CYC + (FIXED if q == "s" else 0.0) if kind == "op" else cycles
-        ops.append((q, kind, fn, reads, writes, extra, busy, late))
+        ops.append((q, kind, fn, reads, writes, extra, busy, late, None))
         return len(ops) - 1
+
+    def either(first, second):
+        first()
+        second()
+        b = ops.pop()
+        a = ops[-1]
+        ops[-1] = a[:3] + (a[3] + [v for v in b[3] if v not in a[3]],) + a[4:8] + ((b[0], b[2], b[6]),)
 
     def ts(out, in0, s1, op0, s2=None, op1=None):
         if op1 is None:
@@ -255,7 +198,7 @@ def rank_program(g, core, T, topo):
 
     def tt(out, in0, in1, op):
         add("v", lambda: g.vector.tensor_tensor(ap(out), ap(in0), ap(in1), op), [in0, in1], [out],
-            width(out) * (1 if SCRATCH[in0[0]][0] == "psum" else 2))
+            width(out) * (1 if "psum" in (SCRATCH[in0[0]][0], SCRATCH[in1[0]][0]) else 2))
 
     def cp(out, in_):
         add("v", lambda: g.vector.tensor_copy(ap(out), ap(in_)), [in_], [out], width(out))
@@ -284,39 +227,43 @@ def rank_program(g, core, T, topo):
         add("p", lambda: g.tensor.matmul_mx(ap(out), ap(lq), ap(ls), ap(rq), ap(rs), start, stop), [lq, ls, rq, rs], [out],
             (width(out) + 16) * 0.6)
 
+    def gather(out, win, off):
+        either(lambda: add("s", lambda: g.scalar.activation(ap(out), ap(win).indirect(ap(off)), act.Copy), [win, off], [out], 80 + 1.5 * width(out)),
+               lambda: add("v", lambda: g.vector.tensor_copy(ap(out), ap(win).indirect(ap(off))), [win, off], [out], 60 + 1.5 * width(out)))
+
     def pick(out, win, off):
-        add("s", lambda: g.scalar.activation(ap(out[1]), ap(win[1]).indirect(ap(off)), act.Copy), [win[1], off], [out[1]],
-            80 + 1.5 * width(out[1]))
+        gather(out[1], win[1], off)
         add("v", lambda: g.vector.tensor_copy(ap(out[0]).bitcast(dt.uint32), ap(win[0]).bitcast(dt.uint32).indirect(ap(off))),
             [win[0], off], [out[0]], 60 + 1.5 * width(out[0]))
 
-    def sgather(out, win, off):
-        add("s", lambda: g.scalar.activation(ap(out), ap(win).indirect(ap(off)), act.Copy), [win, off], [out], 80 + 1.5 * width(out))
-
     def scopy(out, in_, scale=None):
         if scale is None:
-            add("s", lambda: g.scalar.activation(ap(out), ap(in_), act.Copy), [in_], [out], width(out))
+            either(lambda: add("s", lambda: g.scalar.activation(ap(out), ap(in_), act.Copy), [in_], [out], width(out)), lambda: cp(out, in_))
         else:
-            add("s", lambda: g.scalar.activation(ap(out), ap(in_), act.Copy, scale=ap(scale)), [in_, scale], [out], width(out))
+            either(lambda: ts(out, in_, scale, alu.mult),
+                   lambda: add("s", lambda: g.scalar.activation(ap(out), ap(in_), act.Copy, scale=ap(scale)), [in_, scale], [out], width(out)))
 
-    def lin(out, in_, scale=1.0, bias=0.0):
-        if out[0] == "sd1" or (out[0] == "sm" and out[1] % 48 in ONV):
-            return ts(out, in_, scale, alu.mult, bias, alu.add)
-        add("s", lambda: g.scalar.activation(ap(out), ap(in_), act.Identity, bias=sc(bias), scale=sc(scale)),
-            views(in_, scale, bias), [out], width(out))
+    def lin(out, in_, scale=1.0, bias=0.0, soon=False):
+        a = lambda: add("s", lambda: g.scalar.activation(ap(out), ap(in_), act.Identity, bias=sc(bias), scale=sc(scale)),
+                        views(in_, scale, bias), [out], width(out))
+        b = lambda: ts(out, in_, scale, alu.mult, bias, alu.add)
+        either(*((b, a) if soon else (a, b)))
 
-    def side(out, in_):
-        add("s", lambda: g.scalar.activation(ap(out), ap(in_), act.Sign, bias=ap(EDGE)), [in_, EDGE], [out], 1)
+    def total(out, junk, in_, scale):
+        add("s", lambda: g.scalar.activation(ap(junk), ap(in_), act.Identity, scale=scale, accum_out=ap(out)), [in_], [junk, out], 64 + 25)
+
+    def side(out, in_, edge):
+        add("s", lambda: g.scalar.activation(ap(out), ap(in_), act.Sign, bias=ap(edge), scale=2.0), [in_, edge], [out], 1)
 
     def count(junk, in_, last, out, scale=-1.0):
         add("s", lambda: g.scalar.activation(ap(junk), ap(in_), act.Sign, bias=ap(last), scale=sc(scale), accum_out=ap(out)),
             views(in_, last, scale), [junk, out], width(in_) + 25)
 
-    def iota(out, pattern, cm=0):
+    def iota(out, pattern, cm=0, base=0):
         if SCRATCH[out[0]][2] == I32:
-            add("g", lambda: g.iota(ap(out), pattern, 0, cm), [], [out], 160 + 2 * width(out))
+            add("g", lambda: g.iota(ap(out), pattern, base, cm), [], [out], 160 + 2 * width(out))
         else:
-            add("g", lambda: g.iota(ap(out), pattern, 0, cm, allow_small_or_imprecise_dtypes=True), [], [out], 160 + 2 * width(out))
+            add("g", lambda: g.iota(ap(out), pattern, base, cm, allow_small_or_imprecise_dtypes=True), [], [out], 160 + 2 * width(out))
 
     def raw(v):
         return ap(v).bitcast(dt.uint8) if SCRATCH[v[0]][2] == Q4 else ap(v)
@@ -359,35 +306,45 @@ def rank_program(g, core, T, topo):
         lin(quad(v, 1), quad(v, 0))
         lin(half(v, 1), half(v, 0))
 
-    J, J192, J144, BASE, STAY, UNIQ = col("cc", 0), col("cc", 1), col("cc", 2), col("cc", 3), V("cc", 4, 6), col("cc", 6)
-    KF, QF, P32, EDGE, FOUR, N96 = col("cc", 7), col("cc", 8), col("cc", 9), col("cc", 10), col("cc", 11), col("cc", 12)
-    TRI, HALF, S4, J15 = V("tri", 0, 32), V("tri", 32, 64), V("s4", 0, 4), V("s4", 4, 19)
+    J, STAY, UNIQ, P32 = col("cc", 0), V("cc", 4, 6), col("cc", 6), col("cc", 10)
+    PF, KF, QF = col("cc", 7), col("cc", 8), col("cc", 9)
+    EDGE_L, EDGE_R = col("it", 84), col("it", 85)
+    TRI, HALF, S4, J24 = V("tri", 0, 32), V("tri", 32, 64), V("s4", 0, 4), V("s4", 8, 32)
+    WAYS = V("it", 72, 81)
     OE0, FIRST = V("ofs", 144, 150), V("ofs", 152, 164)
+    plus = [("ew1", 0), ("ew2", 0), ("c", 144), ("c", 272)]
+    minus = [("e", 128), ("ew0", 0), ("l", 0), ("f", 0)]
     own0 = me * A
     far0 = A - own0
-    banks = [("psh", 512), ("pss", 0), ("pss", 512)]
+    banks = [[("psd", 512 * b) for b in range(4)], [("pss", 0), ("pss", 512), ("psh", 0), ("psh", 512)]]
 
     def sm(t, i, n=1): return V("sm", 48 * t + i, 48 * t + i + n)
-    def of(t, i, n): return V("ofs", 48 * t + i, 48 * t + i + n)
-    def gg(t, i, n, step=1): return V("gg", 48 * t + i, 48 * t + i + n, step)
+    def sd(k, t, i, n=1, step=1): return V(k, 16 * t + i, 16 * t + i + n, step)
+    def of(t, i, n, step=1): return V("ofs", 48 * t + i, 48 * t + i + n, step)
+    def gg(t, i, n, step=1): return V("gg", 64 * t + i, 64 * t + i + n, step)
     def osrv(t): return of(t, 0, 3)
     def oloc(t): return of(t, 4, 3)
     def oa(t): return of(t, 8, 3)
-    def oe(t): return of(t, 16, 6)
-    def oslot(t): return of(t, 28, 12)
-    def ox(t): return of(t, 40, 3)
-    def num(t): return V("num", 4 * t, 4 * t + 4)
+    def oslot(t): return of(t, 12, 12)
+    def ox(t): return of(t, 24, 12)
+    def oe(t): return of(t, 36, 6)
+    def num(t): return V("nm", 8 * t + 1, 8 * t + 8, 2)
     def ed(t): return pair("ew%d" % t, 128, 224)
     def estat(t): return pair("ew%d" % t, 96, 224)
     def lstat(t): return pair("l", 96 + 96 * t, 224 + 96 * t)
     def slots(t): return pair("win%d" % t, 0, 192)
-    def xs(t, b, k): return V("xp%d" % t, 144 * b + 48 * k, 144 * b + 48 * k + 48)
     def pf(buf, t, c0, c1): return V(buf, PW * t + c0, PW * t + c1)
-    def key(t): return col("so", 8 * t + 6)
-    def won(t): return col("sd0", 8 * t + 6)
-    def zz(t): return sm(t, 12)
+    def note(t): return sd("sd1", t, 1, 3)
+    def spot(t): return sd("sd1", t, 5)
+    def low(t): return sd("sd1", t, 14)
+    def key(t): return sd("so", t, 12)
+    def zz(t): return sm(t, 35)
 
-    def best(ps, buf, stat, t, i, j0):
+    def xs(t, b, k):
+        c = 48 * b if k == 0 else 144 + 96 * b + 48 * k
+        return V("xp%d" % t, c, c + 48)
+
+    def best(ps, buf, stat, t, i, j0, out):
         lo, hi, ml, mh = pf(buf, t, 0, 512), pf(buf, t, 512, 1024), pf(buf, t, 511, 512), pf(buf, t, 1023, 1024)
         pb, cb = pf(buf, t, 1024, 1025), pf(buf, t, 1025, 1026)
         flip = t == 0 and me == 1
@@ -402,26 +359,36 @@ def rank_program(g, core, T, topo):
             ts(sm(t, i + 2), ml, mh, alu.is_ge, -1.0, alu.mult)
             ts(sm(t, i + 3), ml, mh, alu.is_ge, ml, alu.mult)
             count(ja, lo, sm(t, i + 3), cb, sm(t, i + 2))
-            ts(pb, ml, mh, alu.is_lt, sm(t, i + 1), alu.mult)
+            ts(sm(t, i + 4), ml, mh, alu.is_lt, sm(t, i + 1), alu.mult)
+            if out is None:
+                ts(pb, sm(t, i + 4), shift, alu.add)
+            else:
+                ts(out, sm(t, i + 4), cb, alu.add)
             ts(mh, mh, ml, alu.max)
-        else:
+        elif out is None or t == 0:
             scan(lo, V(ps, 0, 512), V("zt", 0, 512), -BIG, alu.max, alu.add)
             count(ja, lo, ml, sm(t, i))
             scan(hi, V(ps, 512, 1024), V("zt", 0, 512), ml, alu.max, alu.add)
             count(jb, hi, mh, cb)
             ts(sm(t, i + 1), ml, mh, alu.is_lt, 512.0, alu.mult)
-            ts(pb, sm(t, i + 1), sm(t, i), alu.max)
+            if out is None:
+                ts(pb, sm(t, i + 1), sm(t, i), alu.max, shift, alu.add)
+            else:
+                ts(out, sm(t, i + 1), sm(t, i), alu.max, cb, alu.add)
+        else:
+            scan(lo, V(ps, 0, 512), V("zt", 0, 512), -BIG, alu.max, alu.add)
+            scan(hi, V(ps, 512, 1024), V("zt", 0, 512), ml, alu.max, alu.add)
+            count(V("jk", j0, j0 + 1024), pf(buf, t, 0, 1024), mh, out)
 
     def send_e(t, land, src):
         calls = [send(peer, [(land[k], src[k])], "ae%d" % t) for k in (0, 1)]
         arrive(peer, list(land), "ae%d" % t, calls)
 
     def serve(t):
-        best("pss", "psv", lstat(t), t, 32, 0)
-        note = V("rm", 3 * t, 3 * t + 3)
-        arrive(peer, [note], "am%d" % t, [send(peer, [(note, pf("psv", t, 1023, 1026))], "am%d" % t)])
+        best("pss", "psv", lstat(t), t, 36, 0, None)
+        arrive(peer, [note(t)], "am%d" % t, [send(peer, [(note(t), pf("psv", t, 1023, 1026))], "am%d" % t)])
         for c in range(3):
-            ts(quad(of(t, c, 1), 0), quad(pf("psv", t, 1024, 1025), c + 1), quad(pf("psv", t, 1025, 1026), c + 1), alu.add)
+            ts(quad(of(t, c, 1), 0), quad(pf("psv", t, 1024, 1025), c + 1), quad(pf("psv", t, 1025, 1026), c + 1), alu.add, -shift, alu.add)
         spread(osrv(t))
         c0 = 96 - 48 * t
         pick(pair("c", c0, c0 + 48), pair("h", 0, 1024), osrv(t))
@@ -430,109 +397,98 @@ def rank_program(g, core, T, topo):
         arrive(peer, land, "ac%d" % t, [call])
 
     def worst(t):
-        mm(V("psh", 0, 192), estat(t), slots(t))
-        tt(V("ad", 0, 192), V("psh", 0, 192), V("pen", 0, 192), alu.add)
-        scan(V("pa", 0, 192), V("ad", 0, 192), V("zt", 0, 192), 2 * BIG, alu.min, alu.add)
-        count(V("jk", 2048, 2240), V("pa", 0, 192), col("pa", 191), sm(t, 13))
+        mm(V("psd", 1536, 1728), estat(t), slots(t))
+        tt(V("ad", 0, 192), V("pen", 0, 192), V("psd", 1536, 1728), alu.subtract)
+        scan(V("pa", 0, 192), V("ad", 0, 192), V("zt", 0, 192), -2 * BIG, alu.max, alu.add)
+        count(V("jk", 2048, 2240), V("pa", 0, 192), col("pa", 191), low(t))
+
+    def near(t):
+        best("psh", "phm", estat(t), t, 41, 1024, spot(t))
+
+    def near_picks(t):
         for c in range(3):
-            lin(quad(gg(t, 36 + c, 1), 0), quad(sm(t, 13), c + 1), -1.0)
-        for q in range(2):
-            cp(quad(oa(t), q), quad(gg(t, 36, 3), 0))
-        cp(half(oa(t), 1), half(oa(t), 0))
+            cp(quad(of(t, 4 + c, 5, 4), 0), quad(sd("sd1", t, 5, 10, 9), c + 1))
+        spread2(of(t, 4, 7))
+        pick(pair("win%d" % t, 192, 240), pair("h", 0, 1024), oloc(t))
         pick(pair("f", 128 + 48 * t, 176 + 48 * t), slots(t), oa(t))
-        ts(sm(t, 16, 4), S4, sm(t, 13), alu.add, 0.0, alu.is_equal)
-        lin(sm(t, 8), sm(t, 13), 1.0, J192)
+        ts(sm(t, 0, 4), num(t), spot(t), alu.is_equal, UNIQ, alu.mult)
+        side(sm(t, 4), spot(t), EDGE_L)
+        total(sd("sd1", t, 12), sm(t, 5, 5), sm(t, 0, 5), 1.0)
+        total(sd("sd1", t, 11), sm(t, 10, 5), sm(t, 0, 5), -1.0)
+        lin(sd("sd1", t, 4), spot(t), -1.0, 0.0, True)
 
     def move(t, k):
-        end = 288 if k == 1 else 240
+        end = 192 + 48 * k
+        to = banks[k - 1]
         for b in range(4):
-            mm(V("psd", 512 * b, 512 * b + 128), pair("k", 512 + 128 * b, 640 + 128 * b), pair("f", 48 + 48 * t, 176 + 48 * t), True, False)
+            mm(V(to[b][0], to[b][1], to[b][1] + 128), pair(minus[b][0], minus[b][1], minus[b][1] + 128), pair("f", 48 + 48 * t, 176 + 48 * t), True, False)
         for b in range(4):
-            mm(V("psd", 512 * b, 512 * b + 128), pair("k", 128 * b, 128 * b + 128), pair("win%d" % t, end - 128, end), False, True)
+            mm(V(to[b][0], to[b][1], to[b][1] + 128), pair(plus[b][0], plus[b][1], plus[b][1] + 128), pair("win%d" % t, end - 128, end), False, True)
         for b in range(4):
-            tt(xs(t, b, k), V("psd", 512 * b + 80, 512 * b + 128), xs(t, b, 0), alu.add)
+            tt(xs(t, b, k), V(to[b][0], to[b][1] + 80, to[b][1] + 128), xs(t, b, 0), alu.add)
         if t + 1 < R:
             for b in range(4):
                 tt(V("et", 192 * (k - 1) + b, 192 * k, 4), V("bi", b, 192, 4), xs(t, b, k), alu.subtract)
 
-    def near(t):
-        best("psh", "phm", estat(t), t, 36, 1024)
-        pb, cb = pf("phm", t, 1024, 1025), pf("phm", t, 1025, 1026)
-        for c in range(3):
-            ts(quad(of(t, 4 + c, 1), 0), quad(pb, c + 1), quad(cb, c + 1), alu.add)
-        spread2(oloc(t))
-        pick(pair("win%d" % t, 192, 240), pair("h", 0, 1024), oloc(t))
-        ts(sm(t, 0), pb, cb, alu.add, float(base_l - base_r), alu.add)
-        side(sm(t, 5), pb)
-        lin(sm(t, 6), sm(t, 5), 1.0, FOUR)
-
-    def near_key(t):
-        ts(sm(t, 20, 4), num(t), sm(t, 0), alu.is_equal)
-        red(sm(t, 7), sm(t, 20, 4), alu.max)
-        lin(col("sd1", 8 * t + 6), sm(t, 7), UNIQ, sm(t, 6))
-        lin(col("sd1", 8 * t + 5), col("sd1", 8 * t + 6), -1.0)
-
     def y_out(t):
         for o in range(O):
-            mm(V(banks[o][0], banks[o][1], banks[o][1] + 192), pair("w", 128 * o, 128 * o + 128), slots(t + 1))
+            mm(V("psd", 512 * o, 512 * o + 192), pair("w", 128 * o, 128 * o + 128), slots(t + 1))
         for o in range(O):
             c = (t * O + o) * 192
-            (cp if t == R - 1 and o == 1 else scopy)(V("ys", c, c + 192), V(banks[o][0], banks[o][1], banks[o][1] + 192))
+            scopy(V("ys", c, c + 192), V("psd", 512 * o, 512 * o + 192))
         c = 576 * t
         if t + 1 < R:
-            store("y", T.y[:, c:c + 576], V("ys", c, c + 576), [V("rm", 3 * t + 3, 3 * t + 6)])
+            store("y", T.y[:, c:c + 576], V("ys", c, c + 576), [note(t + 1)])
         else:
-            store("y", T.y[:, c:c + 384], V("ys", c, c + 384))
-            store("y", T.y[:, c + 384:c + 576], V("ys", c + 384, c + 576))
+            for o in range(O):
+                store("y", T.y[:, c + 192 * o:c + 192 * o + 192], V("ys", c + 192 * o, c + 192 * o + 192))
 
     def decide(t):
-        mr, pb, cb = col("rm", 3 * t), col("rm", 3 * t + 1), col("rm", 3 * t + 2)
-        ts(won(t), mr, pf("phm", t, 1023, 1024), alu.is_gt if base_r > base_l else alu.is_ge)
-        ts(V("sd1", 8 * t, 8 * t + 4), num(t), pb, alu.subtract, cb, alu.is_equal)
-        side(col("sd1", 8 * t + 4), pb)
-        scan(V("so", 8 * t, 8 * t + 7), V("sd0", 8 * t, 8 * t + 7), V("sd1", 8 * t, 8 * t + 7), 0.0, alu.mult, alu.add)
+        last = t + 1 == R
+        mr, pb, cb, won = sd("sd1", t, 1), sd("sd1", t, 2), sd("sd1", t, 3), col("sd0", 5)
+        ts(V("sd0", 5, 13, 7), V("zt", 0, 2), mr, alu.add, pf("phm", t, 1023, 1024), alu.is_gt if base_r > base_l else alu.is_ge)
+        ts(sd("sd1", t, 6, 4), num(t), pb, alu.subtract, cb, alu.is_equal)
+        either(lambda: side(sd("sd1", t, 10), pb, EDGE_R), lambda: ts(sd("sd1", t, 10), pb, A - 0.5 - shift, alu.is_gt, 1.0, alu.add))
+        scan(sd("so", t, 2, 12), V("sd0", 2, 14), sd("sd1", t, 2, 12), 0.0, alu.mult, alu.add)
         scopy(quad(V("uu", 32, 64), 2), quad(HALF, 1), quad(key(t), 1))
-        ts(V("uu", 0, 32), TRI, key(t), alu.mult)
+        scopy(V("uu", 0, 32), TRI, key(t))
         scopy(quad(V("uu", 32, 64), 3), quad(HALF, 2), quad(key(t), 2))
-        ts(quad(V("uu", 64, 96), 3), quad(HALF, 1), quad(key(t), 1), alu.mult)
+        scopy(quad(V("uu", 64, 96), 3), quad(HALF, 1), quad(key(t), 1))
         tr(V("kk", 0, 96), V("uu", 0, 96))
         ts(V("sam", 0, 96), V("kk", 0, 96), key(t), alu.is_equal, -1000.0, alu.mult)
         red(zz(t), V("sam", 0, 97), alu.add)
-        if t + 1 < R:
-            lin(sm(t, 2), won(t), -48.0, J144)
+        lin(sm(t, 33), won, 48.0, 0.0, True)
+        lin(sm(t, 24, 9), WAYS, 1.0, sm(t, 33), True)
+        ts(sm(t, 16, 4), S4, low(t), alu.is_equal, sd("so", t, 13), alu.mult)
+        tt(sm(t, 20, 4), sm(t, 16, 4), sm(t, 29, 4), alu.min)
+        if not last:
             for c in range(3):
-                ts(quad(of(t, 16 + 2 * c, 2), 0), quad(STAY, c + 1), quad(zz(t), c + 1), alu.max, quad(sm(t, 2), c + 1), alu.min)
+                ts(quad(of(t, 36 + 2 * c, 2), 0), quad(STAY, c + 1), quad(zz(t), c + 1), alu.max, quad(sm(t, 28), c + 1), alu.min)
             spread(oe(t))
             quant("ew%d" % t, 224, 352, V("et", 0, 512))
             pick(ed(t + 1), pair("ew%d" % t, 128, 352), oe(t))
             send_e(t + 1, pair("l", 224 + 96 * t, 320 + 96 * t), ed(t + 1))
-        lin(sm(t, 9), won(t), 48.0, sm(t, 8))
-        ts(sm(t, 10), key(t), float(CAPP), alu.is_lt, sm(t, 9), alu.mult)
-        lin(sm(t, 24, 4), sm(t, 16, 4), sm(t, 10))
-        lin(sm(t, 28), won(t), -48.0, N96)
-        both = of(t, 28, 15)
-        ts(sm(t, 4), zz(t), 0.0, alu.is_gt)
         for c in range(3):
-            ts(quad(gg(t, c, 15 - c, 3), 0), quad(sm(t, 24, 5), c + 1), quad(zz(t), c + 1), alu.min, 0.0, alu.max)
-        tt(quad(gg(t, 16, 15), 0), quad(gg(t, 0, 15), 0), quad(J15, 0), alu.add)
-        for q in range(2 if t + 1 < R else 4):
-            cp(quad(both, q), quad(gg(t, 16, 15), 0))
-        if t + 1 < R:
+            ts(quad(gg(t, c, 24 - c, 3), 0), quad(sm(t, 20, 8), c + 1), quad(zz(t), c + 1), alu.min, 0.0, alu.max)
+        tt(quad(gg(t, 32, 24), 0), quad(gg(t, 0, 24), 0), quad(J24, 0), alu.add)
+        both = of(t, 12, 24)
+        for q in range(4 if last else 2):
+            cp(quad(both, q), quad(gg(t, 32, 24), 0))
+        if not last:
             cp(half(both, 1), half(both, 0))
         pick(slots(t + 1), pair("win%d" % t, 0, 288), oslot(t))
-        for b in range(4):
-            sgather(xs(t + 1, b, 0) if t + 1 < R else V("pxs", b, 192, 4), V("xp%d" % t, 144 * b, 144 * b + 144), ox(t))
-        ts(sm(t, 11), pb, cb, alu.add, sm(t, 0), alu.subtract)
-        lin(sm(t, 15), sm(t, 11), won(t), sm(t, 0))
-        ts(sm(t, 14), key(t), float(CAPP), alu.is_lt, -1.0, alu.mult)
-        ts(sm(t, 20, 4), num(t), sm(t, 15), alu.subtract, sm(t, 14), alu.mult)
-        tt(sm(t, 40, 4), sm(t, 20, 4), sm(t, 16, 4), alu.mult)
-        lin(sm(t, 44, 4), sm(t, 40, 4), sm(t, 4), 0.0 if t + 1 < R else BASE)
-        if t + 1 < R:
-            tt(num(t + 1), num(t), sm(t, 44, 4), alu.add)
+        if not last:
+            gather(V("xp%d" % (t + 1), 0, 192), V("xp%d" % t, 0, 576), ox(t))
         else:
+            for b in range(4):
+                u = b % 2
+                gather(V("pxs", 64 - 64 * u + b, 256, 4), V("xp%d" % t, 0, 576), of(t, 24 + 3 * b - u, 3 + u))
+        lin(V("nm", 8 * t, 8 * t + 8, 2), num(t), -1.0, sd("so", t, 5), True)
+        ts(V("rr", 1, 8, 2), sm(t, 20, 4), zz(t), alu.min, 0.0, alu.is_gt)
+        scan(V("nm", 8 * t + 8, 8 * t + 16), V("rr", 0, 8), V("nm", 8 * t, 8 * t + 8), 0.0, alu.mult, alu.add)
+        if last:
             for c in range(3):
-                tt(quad(V("nt", c, 12, 3), 0), quad(num(t), c + 1), quad(sm(t, 44, 4), c + 1), alu.add)
+                lin(quad(V("nt", c, 12, 3), 0), quad(num(R), c + 1), 1.0, quad(col("it", 86), c + 1), True)
 
     small = [load("y", V("xi", 0, 192), T.x[:, :]), load("s", V("bi", 0, 192), T.b[:, :])]
     first = load("y", V("di", 0, 4 * CUT), T.d[:, 0:4 * CUT], (), small)
@@ -542,29 +498,43 @@ def rank_program(g, core, T, topo):
     iota(col("pi", 0), [[0, 1]], 1)
     iota(V("it", 0, 6), [[16, 3], [0, 2]])
     iota(V("it", 8, 40), [[0, 2], [1, 16]])
-    iota(V("it", 40, 44), [[48, 4]])
-    iota(V("it", 44, 56), [[16, 12]])
-    iota(V("ip", 0, 192), [[0, 4], [1, 48]])
+    iota(V("it", 40, 44), [[48, 4]], 0, -16)
+    iota(V("it", 48, 72), [[0, 2], [16, 12]])
+    iota(V("it", 72, 76), [[48, 4]], 0, 192)
+    iota(V("it", 77, 81), [[-48, 4]], 0, 192)
+    iota(V("it", 82, 84), [[0, 2]], 0, -32)
+    iota(V("it", 84, 86), [[2 * int(shift), 2]], 0, 1 - 2 * A)
+    iota(V("it", 86, 88), [[rank * A - 2 * base_l, 2]], 0, base_l)
+    iota(V("sd0", 0, 16), [[0, 16]], 0, 1)
+    iota(V("sd0", 2, 7, 4), [[0, 2]], 0, 0)
+    iota(V("sd0", 11, 14, 2), [[-203, 2]], 0, 3)
+    iota(V("sd1", 13, 48, 16), [[0, 3]], 0, 200 * CAPP)
+    iota(col("sam", 96), [[0, 1]], 0, 1000 * CAPP - 500)
+    iota(V("ip", 0, 192), [[0, 4], [1, 48]], 0, 16)
     iota(V("idn", 0, 128), [[-1, 128]], 1)
     ms(V("zt", 0, 576), 0.0)
+    ms(V("ofs", 7, 144, 48), 0)
     lin(V("et", 192, 512), V("zt", 0, 320))
     ts(col("pi", 1), col("pi", 0), 15, alu.bitwise_and)
-    ts(col("pi", 2), col("pi", 0), 5, alu.arith_shift_right)
-    ts(col("pi", 3), col("pi", 0), 31, alu.bitwise_and)
-    for name in ("ew0", "l", "f", "ew1", "ew2"):
-        quant(name, 0, 128, V("zt", 0, 512))
-    quant("e", 128, 256, V("zt", 0, 512))
-    quant("c", 144, 288, V("zt", 0, 576))
-    cp(KF, col("pi", 1))
-    ts(QF, col("pi", 2), 16.0, alu.mult, -16.0, alu.add)
-    cp(P32, col("pi", 3))
+    ts(col("pi", 2), col("pi", 0), 1, alu.arith_shift_right, 48, alu.bitwise_and)
+    cp(V("cc", 7, 10), V("pi", 0, 3))
+    lin(P32, QF, -2.0, PF)
     ts(OE0, V("it", 0, 6), KF, alu.add)
-    ts(J, KF, QF, alu.add)
-    for i in range(4):
+    lin(J, KF, 1.0, QF)
+    for i in range(2):
         lin(V("ct", 516 * i, 516 * i + 516), V("zt", 0, 516))
     ts(V("idn", 128, 256), V("idn", 0, 128), 0.0, alu.is_equal)
+    for tiles, c in ((minus, -0.25), (plus, 0.25)):
+        for i in range(2):
+            lo = 516 * i + 2 + i
+            lin(V("ct", lo, lo + 512, 4), V("idn", 128, 256), c)
+        for b in range(4):
+            lo = 516 * (b % 2) + 2 + b % 2 - b
+            quant(tiles[b][0], tiles[b][1], tiles[b][1] + 128, V("ct", lo, lo + 512))
     tt(V("et", 0, 192), V("bi", 0, 192), V("xi", 0, 192), alu.subtract)
-    ts(V("pen", 0, 192), V("ip", 0, 192), J, alu.not_equal, BIG, alu.mult)
+    lin(V("ad", 0, 192), V("ip", 0, 192), -1.0, J)
+    add("s", lambda: g.scalar.activation(ap(V("pa", 0, 192)), ap(V("ad", 0, 192)), act.Abs), [V("ad", 0, 192)], [V("pa", 0, 192)], 192)
+    lin(V("pen", 0, 192), V("pa", 0, 192), -BIG / 128)
     quant("e", 0, 128, V("et", 0, 512))
     land = [V("mq", 0, 48), V("ms", 0, 192)]
     arrive(peer, land, "ae0", [send(peer, [(land[0], V("eq", 0, 48)), (land[1], V("es", 0, 192))], "ae0")])
@@ -572,9 +542,6 @@ def rank_program(g, core, T, topo):
     pick(pair("l", 128, 224), pair("m", 0, 48), OE0)
     for b in range(4):
         scopy(xs(0, b, 0), V("xi", b, 192, 4))
-    for i in range(4):
-        lo = 516 * i + 2 + i % 2
-        lin(V("ct", lo, lo + 512, 4), V("idn", 128, 256), 0.25 if i < 2 else -0.25)
     quant("h", own0, own0 + CUT, V("di", 0, 4 * CUT))
     quant("h", own0 + CUT, own0 + A, V("di", 4 * CUT, 2048))
     v, u, s = V("hq", own0, own0 + CUT), V("hq", own0 + CUT, own0 + A), V("hs", own0, own0 + A)
@@ -583,33 +550,22 @@ def rank_program(g, core, T, topo):
     cp(quad(V("af", 0, 12), 0), quad(V("ai", 0, 12), 0))
     sspread(V("af", 0, 12))
     cp(FIRST, V("af", 0, 12))
-    for s in (1, 0):
-        for b in range(4):
-            lo = 516 * (2 * s + b % 2) + 2 + b % 2 - b
-            quant("k", 512 * s + 128 * b, 512 * s + 128 * b + 128, V("ct", lo, lo + 512))
     pick(slots(0), pair("h", own0, own0 + A), FIRST)
     lin(quad(num(0), 0), quad(V("zt", 0, 4), 0))
     for c in range(3):
-        ts(quad(num(0), c + 1), quad(V("af", c, 12, 3), 0), float(rank * A - base_r), alu.add)
+        lin(quad(num(0), c + 1), quad(V("af", c, 12, 3), 0), 1.0, quad(col("it", 87), 0))
     lin(S4, V("it", 40, 44), 1.0, J)
-    ts(J192, J, 192.0, alu.add)
-    ts(J144, J, 144.0, alu.add)
-    ts(UNIQ, J, 8.0, alu.mult, 16.0, alu.add)
-    ts(STAY, V("it", 0, 2), QF, alu.add, J, alu.add)
+    lin(J24, V("it", 48, 72), 1.0, KF)
+    lin(UNIQ, J, 8.0)
+    lin(col("cc", 1), J, 1.0, QF)
+    lin(STAY, V("it", 82, 84), 1.0, col("cc", 1))
+    lin(col("it", 76), col("s4", 2))
     ts(TRI, V("it", 8, 40), P32, alu.is_gt)
     ts(HALF, V("it", 8, 40), 15.5, alu.max, P32, alu.is_gt)
-    lin(V("s4", 4, 16), V("it", 44, 56), 1.0, KF)
-    lin(V("s4", 16, 19), V("it", 44, 47), 1.0, KF)
-    ms(BASE, float(base_r))
-    ms(EDGE, 0.5 - A)
-    ms(FOUR, 4.0)
-    ms(N96, 96.0)
-    ms(V("sd0", 0, 24), 1.0)
+    lin(col("sd0", 10), UNIQ)
+    lin(V("rr", 0, 8), V("zt", 0, 8))
     lin(V("uu", 32, 96), V("zt", 0, 64))
-    ms(col("sam", 96), 1000.0 * CAPP - 500.0)
     lin(quad(V("nt", 12, 32), 0), quad(V("zt", 0, 20), 0))
-    lin(V("sd0", 0, 24, 8), V("zt", 0, 3))
-    lin(V("sd0", 4, 24, 8), V("zt", 0, 3), 1.0, UNIQ)
 
     for t in range(R):
         if t == 0:
@@ -617,22 +573,22 @@ def rank_program(g, core, T, topo):
         near(t)
         serve(t)
         if t == 0:
-            load("y", V("wi", 0, 1536), T.w[:, :], [V("rm", 0, 3)])
+            load("y", V("wi", 0, 1536), T.w[:, :], [note(0)])
             for o in range(O):
                 quant("w", 128 * o, 128 * o + 128, V("wi", 512 * o, 512 * o + 512))
         else:
             worst(t)
             y_out(t - 1)
-        near_key(t)
-        move(t, 2)
+        near_picks(t)
         move(t, 1)
+        move(t, 2)
         decide(t)
 
     y_out(R - 1)
     store("y", T.oc[:, :], slots(R)[0])
     for k in range(4):
         store("ys"[k % 2], T.osc[4 * k:4 * k + 4, :], V("win%ds" % R, 0, 192, 1, 32 * k, 32 * k + 4))
-    store("s", T.px[:, :], V("pxs", 0, 192))
+    store("s", T.px[:, :], V("pxs", 64, 256))
     tr(quad(V("nt", 32, 64), 0), quad(V("nt", 0, 32), 0))
     store("y", T.an[:, :], V("nt", 32, 48, 1, 0, 12))
-    emit(g, T, ops)
+    emit(g, T, ops, me)

import numpy as np
from concourse.bass import DstId, RemoteDMATransfer
from concourse.mybir import dt, AluOpType, AxisListType, ActivationFunctionType

A, M, CAPP, R, O = 512, 48, 8, 3, 3
F32, BF, I32, U16, Q4, U8 = "float32", "bfloat16", "int32", "uint16", "float8_e4m3fn_x4", "uint8"
PW = 1026
BIG = 1.0e29
CUT = 384

SCRATCH = {
    "xi": ("sbuf", [128, 192], BF), "bi": ("sbuf", [128, 192], BF), "di": ("sbuf", [128, 2048], BF),
    "wi": ("sbuf", [128, 1536], BF), "ai": ("sbuf", [128, 12], I32), "af": ("sbuf", [128, 12], F32),
    "zt": ("sbuf", [128, 576], BF), "et": ("sbuf", [128, 512], BF), "ct": ("sbuf", [128, 1032], BF),
    "pi": ("sbuf", [128, 4], I32), "cc": ("sbuf", [128, 16], F32), "it": ("sbuf", [128, 96], F32),
    "ip": ("sbuf", [128, 192], F32), "idn": ("sbuf", [128, 256], F32),
    "tri": ("sbuf", [128, 64], F32), "s4": ("sbuf", [128, 40], F32), "pen": ("sbuf", [128, 192], F32),
    "psv": ("sbuf", [128, 3 * PW], F32), "phm": ("sbuf", [128, 3 * PW], F32),
    "jk": ("sbuf", [128, 2240], BF), "ad": ("sbuf", [128, 192], F32), "pa": ("sbuf", [128, 192], F32),
    "sm": ("sbuf", [128, 144], F32), "nm": ("sbuf", [128, 32], F32), "rr": ("sbuf", [128, 8], F32), "nt": ("sbuf", [128, 64], F32),
    "sd0": ("sbuf", [128, 16], F32), "sd1": ("sbuf", [128, 48], F32), "so": ("sbuf", [128, 48], F32),
    "uu": ("sbuf", [128, 96], F32), "kk": ("sbuf", [128, 96], F32), "sam": ("sbuf", [128, 97], F32),
    "gg": ("sbuf", [128, 192], F32), "ofs": ("sbuf", [128, 176], U16),
    "xp0": ("sbuf", [128, 576], BF), "xp1": ("sbuf", [128, 576], BF), "xp2": ("sbuf", [128, 576], BF),
    "pxs": ("sbuf", [128, 256], F32), "ys": ("sbuf", [128, 1728], F32),
    "pss": ("psum", [128, 1024], F32), "psh": ("psum", [128, 1024], F32), "psd": ("psum", [128, 2048], F32),
}
for _n, _w in (("h", 1024), ("w", 384), ("e", 256), ("m", 192), ("l", 416), ("c", 400), ("f", 272),
               ("ew0", 352), ("ew1", 352), ("ew2", 224), ("win0", 432), ("win1", 432), ("win2", 432), ("win3", 192)):
    SCRATCH[_n + "q"] = ("sbuf", [128, _w], Q4)
    SCRATCH[_n + "s"] = ("sbuf", [128, _w], U8)

NDMA = 20
SEMAPHORES = (["cv", "cs", "cp", "cg", "sent", "ah0", "ah1"] + ["ae%d" % t for t in range(R)]
              + ["am%d" % t for t in range(R)] + ["ac%d" % t for t in range(R)] + ["dm%d" % i for i in range(NDMA)])
ENG = {"v": "cv", "s": "cs", "p": "cp", "g": "cg"}
CYC, CALL, ROW, RATE, FIXED = 0.9, 350.0, 1.0, 500.0, 60.0
DIGITS = "0123456789abcdefghijklmnopqrstuvwxyzABCDEFGHIJKLMNOPQRSTUVWXYZ"
ORDER = (
    "02000c0K04060I080S0Q0a120e0G160U110W0g19140k1c1g0i0w0O2I0Y0s0M0C1a1k1y1w2o2A1e1E1G1A1K200u1M221C242c1i1s32282e2u1o1m0y0E360q2g1I2q0A1O0o1Q0m2i1u3i2k2m26383m2U2a3k2W1q3o342Y3q303a3s3u3c3w2K1Z3y3C3G3E1X3e3M3I3K2t3g3Q3O442Q46481S4m4u4o3S1U4a2x2N4q3A4s4c3W5D5A5y4i4k4g4e5E5V4w4y5I5N4G5K2G5G4A5Y2C4E4I4O5O4C2E4M3U58524Q2O4K4W542y5Q5a5X4U5c4S5g4Y565S5e5i5k505o5m5q5s5w5u6662646e686a6c606g6i6u6L6q6s6k6Q6w6M6m6S6A6y6C6U6E3Y6I6W6o6G706Y407E74726O78767G7a7c7I7e428i7K7g7m7k8k7o7O7M7Q828o7s7q8r7u807S847y8m7U867x887A7i8g8e8c8a9z9w7W9u8y8u8C9A8s8A7Y928K8w9F9D9G8E9I948I9R8G8S909U9K8M9T8Q8O7C9M8U9c8W989a9O8Y9k969g9Y9ia2a09e9s9q9o9ma8a6a4aa9WaeacamaHaqao2TagaMasaIaiaOauawaQayaKaSaAaCakaUaWbIaYb0bMbAbKb4b2bCb6b8cmbEbacebRbGbcbibkbgcgbSc0bWbObYbmbockbqaEc2btcic4buccbebwdebUdcdac8dxdgdjdmdodkcadyc6dqe7dAcQcqcMdscudCcocybyducUcCcScsdIdGcOdEcAe8d0cYdKcweacWdOefdMdQdScGdUdWd2cEcKd8eAd4eIekcIeCedeieGeEemerd6epewete2egdYeue5e0eyeMeOeK",
    "02000K0c04060I080S0M14130e0k0G160Q0P180u0U1a0w1c0s100a0Y1g1y0g0A1k2B1w1Y1A0W1e1U1E1G1K202o1W1C222M1M242c1i281o322e1s2s1m0o2u0i2g362C0q1I0y1O1Q2i1u3q2k2m26383u2U2a3s2W2I3w343A1S2w3y3C3E3I3c3G3K3M2q3g3e3W3O3U3S3i3a2Y0m0C403k423Y301q3m44464C4E4m4L4k484o3o2K4I3Q4G4q0E2G4c5Q5O2Q5T4s6a5U4y4A4u625Y5W6d604Q2O4w4M2E4O2y646e4W4a4Y4U664S6g5054565o525i685m5c5k585s5e5q5a5w6i5u5g5A5y6k5C6m5E5I5G5K5M6o6s6q6u6G6K6I6w6y6M6A766O6Q4g6C786S7a6Y6W6U7c7U6E7W7e7g70727i7Y7k74807o7m8k8i8g4i7q7s8m867u8o4e8y8u7w7C7A7E82847I7K887G8w8q7O8A9i7N8a9e8s8I8d8E7Q8H8C8K8S7y8M8Q9O8e9K9k9M8U908O8Wa79g9Q989T9U9Y9W922Sa98Ya094967Sa29a9c9q9oa49s9m9y9wag9Aaeai9u9G9I9E9CakamaoaqaaauasacaXawb2aEaCaGayb4aIb6aMaKb8aOaAbaaRbcbebgaYbibkaSbmb0bocCbQc2bqcucwbYbSc0bsc8bybAbwc4bUcAbEbGcybCbWbKc6bJccbMbuducadqdscecgdNdwcidFdCdAdPdyckdQdGcqcscmdIbOdSaUd4cEcGdKcKcodUdWdYcSeocOcIcQe0dcemd8cMd6e8e4dge2dee6cWd2eaeccUdkdmdoeQcYeYeAeSeUdaeWeyeCeHdieEd0eMeIeheieKeqeleOefexeuesf0f2f4",
)


def V(name, c0, c1, step=1, p0=0, p1=128):
    return (name, c0, c1, step, p0, p1)


def col(name, c):
    return (name, c, c + 1, 1, 0, 128)


def quad(v, q):
    return (v[0], v[1], v[2], v[3], 32 * q, 32 * q + 32)


def half(v, h):
    return (v[0], v[1], v[2], v[3], 64 * h, 64 * h + 64)


def width(v):
    return len(range(v[1], v[2], v[3]))


def depend(ops):
    lastw, lastr, out = {}, {}, []

    def cells(v):
        name, c0, c1, step, p0, p1 = v
        if SCRATCH[name][0] == "psum":
            return (slice(0, 128), slice(c0 // 512 * 512, -(-c1 // 512) * 512))
        return (slice(p0, p1), slice(c0, c1, step))

    for i, (q, kind, fn, reads, writes, extra, busy, late, alt) in enumerate(ops):
        deps, order = set(), set()
        for v in list(reads) + list(writes):
            if v[0] not in lastw:
                lastw[v[0]] = np.full(SCRATCH[v[0]][1], -1, np.int32)
                lastr[v[0]] = []
        for v in reads:
            deps.update(np.unique(lastw[v[0]][cells(v)]).tolist())
        for v in list(writes) + [v for v in reads if SCRATCH[v[0]][0] == "psum"]:
            for j, a in lastr[v[0]]:
                if a[cells(v)].any() and (v in writes or ops[j][0] != q or alt or ops[j][8]):
                    deps.add(j)
        for v in writes:
            for j in np.unique(lastw[v[0]][cells(v)]).tolist():
                (order if j >= 0 and q == "p" and ops[j][0] == "p" else deps).add(j)
        deps.discard(-1)
        deps.discard(i)
        if kind == "ext":
            order.update(extra[2])
        if kind == "dma":
            order.update(extra)
        out.append((deps, order))
        for v in writes:
            lastw[v[0]][cells(v)] = i
            for j, a in lastr[v[0]]:
                a[cells(v)] = False
            lastr[v[0]] = [(j, a) for j, a in lastr[v[0]] if a.any()]
        for v in reads:
            a = np.zeros(SCRATCH[v[0]][1], bool)
            a[cells(v)] = True
            lastr[v[0]].append((i, a))
    return out


def emit(g, T, ops, me):
    queues = {"v": g.vector, "s": g.scalar, "p": g.tensor, "g": g, "y": g.sync}
    dep = depend(ops)
    text = ORDER[me]
    plan = [divmod(62 * DIGITS.index(text[k]) + DIGITS.index(text[k + 1]), 2) for k in range(0, len(text), 2)]
    plan = plan or [(i, 0) for i in range(len(ops))]
    assert sorted(i for i, w in plan) == list(range(len(ops)))
    count, known, token, seen, total, place = {}, {k: {} for k in queues}, {}, {}, {}, {}
    ndma = 0
    for i, other in plan:
        q, kind, fn, reads, writes, extra = ops[i][:6]
        if other:
            q, fn = ops[i][8][:2]
        assert all(j in place for j in dep[i][0] | dep[i][1])
        place[i] = len(place)
        if kind == "ext":
            token[i], seen[i] = extra[:2], {}
            total[extra[0]] = extra[1]
            continue
        kn = known[q]
        for j in sorted(dep[i][0], key=lambda j: -place[j]):
            s, n = token[j]
            if kn.get(s, 0) < n:
                queues[q].wait_ge(T.sem[s], n)
                kn[s] = n
                for s2, n2 in seen[j].items():
                    kn[s2] = max(kn.get(s2, 0), n2)
        seen[i] = dict(kn)
        if kind == "remote":
            fn()
            total["sent"] = total.get("sent", 0) + extra
        elif kind == "dma":
            s = "dm%d" % ndma
            ndma += 1
            fn(queues[q]).then_inc(T.sem[s], 16)
            total[s] = 16
            token[i] = (s, 16)
        else:
            s = ENG[q]
            count[s] = count.get(s, 0) + 1
            fn().then_inc(T.sem[s], 1)
            total[s] = count[s]
            token[i] = (s, count[s])
    for s, n in total.items():
        if known["g"].get(s, 0) < n:
            g.wait_ge(T.sem[s], n)


def rank_program(g, core, T, topo):
    rank = T.rank_of(core)
    if rank is None:
        return
    cores = list(T.cores)
    mine = [r for r in range(len(cores)) if topo.die(cores[r]) == topo.die(core)]
    other = [r for r in range(len(cores)) if r not in mine]
    assert len(mine) == 2 and len(other) == 2 and mine[1] == mine[0] + 1 and other[1] == other[0] + 1
    me = mine.index(rank)
    mate, peer = cores[mine[1 - me]], cores[other[me]]
    base_l, base_r = mine[0] * A, other[0] * A
    shift = float(base_l - base_r)
    ops = []
    alu, act = AluOpType, ActivationFunctionType

    def ap(v):
        name, c0, c1, step, p0, p1 = v
        return T[name][p0:p1, c0:c1] if step == 1 else T[name][p0:p1, c0:c1:step]

    def sc(x):
        return ap(x) if isinstance(x, tuple) else x

    def views(*xs):
        return [x for x in xs if isinstance(x, tuple)]

    def add(q, fn, reads, writes, cycles, kind="op", extra=None, late=0.0):
        busy = max(cycles, 64) * CYC + (FIXED if q == "s" else 0.0) if kind == "op" else cycles
        ops.append((q, kind, fn, reads, writes, extra, busy, late, None))
        return len(ops) - 1

    def either(first, second):
        first()
        second()
        b = ops.pop()
        a = ops[-1]
        ops[-1] = a[:3] + (a[3] + [v for v in b[3] if v not in a[3]],) + a[4:8] + ((b[0], b[2], b[6]),)

    def ts(out, in0, s1, op0, s2=None, op1=None):
        if op1 is None:
            add("v", lambda: g.vector.tensor_scalar(ap(out), ap(in0), sc(s1), None, op0), views(in0, s1), [out], width(out))
        else:
            add("v", lambda: g.vector.tensor_scalar(ap(out), ap(in0), sc(s1), sc(s2), op0, op1), views(in0, s1, s2), [out], width(out))

    def tt(out, in0, in1, op):
        add("v", lambda: g.vector.tensor_tensor(ap(out), ap(in0), ap(in1), op), [in0, in1], [out],
            width(out) * (1 if "psum" in (SCRATCH[in0[0]][0], SCRATCH[in1[0]][0]) else 2))

    def cp(out, in_):
        add("v", lambda: g.vector.tensor_copy(ap(out), ap(in_)), [in_], [out], width(out))

    def ms(out, c):
        add("v", lambda: g.vector.memset(ap(out), c), [], [out], width(out) // (2 if SCRATCH[out[0]][2] == BF else 1))

    def red(out, in_, op):
        add("v", lambda: g.vector.tensor_reduce(ap(out), ap(in_), AxisListType.X, op), [in_], [out], width(in_))

    def scan(out, d0, d1, init, op0, op1):
        add("v", lambda: g.vector.tensor_tensor_scan(ap(out), ap(d0), ap(d1), sc(init), op0, op1), views(d0, d1, init), [out], width(out))

    def tr(out, in_):
        add("v", lambda: g.vector.transpose(ap(out), ap(in_)), [in_], [out], width(out))

    def pair(name, c0, c1):
        return V(name + "q", c0, c1), V(name + "s", c0, c1)

    def quant(name, c0, c1, in_):
        q, s = pair(name, c0, c1)
        add("v", lambda: g.vector.quantize_mx(ap(q), ap(s), ap(in_)), [in_], [q, s], 15 + width(in_) * 0.27)

    def mm(out, lhs, rhs, start=True, stop=True):
        (lq, ls), (rq, rs) = lhs, rhs
        add("p", lambda: g.tensor.matmul_mx(ap(out), ap(lq), ap(ls), ap(rq), ap(rs), start, stop), [lq, ls, rq, rs], [out],
            (width(out) + 16) * 0.6)

    def gather(out, win, off):
        either(lambda: add("s", lambda: g.scalar.activation(ap(out), ap(win).indirect(ap(off)), act.Copy), [win, off], [out], 80 + 1.5 * width(out)),
               lambda: add("v", lambda: g.vector.tensor_copy(ap(out), ap(win).indirect(ap(off))), [win, off], [out], 60 + 1.5 * width(out)))

    def pick(out, win, off):
        gather(out[1], win[1], off)
        add("v", lambda: g.vector.tensor_copy(ap(out[0]).bitcast(dt.uint32), ap(win[0]).bitcast(dt.uint32).indirect(ap(off))),
            [win[0], off], [out[0]], 60 + 1.5 * width(out[0]))

    def scopy(out, in_, scale=None):
        if scale is None:
            either(lambda: add("s", lambda: g.scalar.activation(ap(out), ap(in_), act.Copy), [in_], [out], width(out)), lambda: cp(out, in_))
        else:
            either(lambda: ts(out, in_, scale, alu.mult),
                   lambda: add("s", lambda: g.scalar.activation(ap(out), ap(in_), act.Copy, scale=ap(scale)), [in_, scale], [out], width(out)))

    def lin(out, in_, scale=1.0, bias=0.0, soon=False):
        a = lambda: add("s", lambda: g.scalar.activation(ap(out), ap(in_), act.Identity, bias=sc(bias), scale=sc(scale)),
                        views(in_, scale, bias), [out], width(out))
        b = lambda: ts(out, in_, scale, alu.mult, bias, alu.add)
        either(*((b, a) if soon else (a, b)))

    def total(out, junk, in_, scale):
        add("s", lambda: g.scalar.activation(ap(junk), ap(in_), act.Identity, scale=scale, accum_out=ap(out)), [in_], [junk, out], 64 + 25)

    def side(out, in_, edge):
        add("s", lambda: g.scalar.activation(ap(out), ap(in_), act.Sign, bias=ap(edge), scale=2.0), [in_, edge], [out], 1)

    def count(junk, in_, last, out, scale=-1.0):
        add("s", lambda: g.scalar.activation(ap(junk), ap(in_), act.Sign, bias=ap(last), scale=sc(scale), accum_out=ap(out)),
            views(in_, last, scale), [junk, out], width(in_) + 25)

    def iota(out, pattern, cm=0, base=0):
        if SCRATCH[out[0]][2] == I32:
            add("g", lambda: g.iota(ap(out), pattern, base, cm), [], [out], 160 + 2 * width(out))
        else:
            add("g", lambda: g.iota(ap(out), pattern, base, cm, allow_small_or_imprecise_dtypes=True), [], [out], 160 + 2 * width(out))

    def raw(v):
        return ap(v).bitcast(dt.uint8) if SCRATCH[v[0]][2] == Q4 else ap(v)

    def moved(v):
        return (v[5] - v[4]) * (ROW + width(v) * {F32: 4, I32: 4, Q4: 4, BF: 2, U16: 2, U8: 1}[SCRATCH[v[0]][2]] / RATE)

    def load(q, out, src, after=(), behind=()):
        return add(q, lambda e: e.dma_start(ap(out), src), list(after), [out], 100.0, "dma", list(behind), moved(out))

    def store(q, dst, in_, after=()):
        add(q, lambda e: e.dma_start(dst, raw(in_)), [in_] + list(after), [], 100.0, "dma", [], moved(in_))

    def send(dst, moves, sem):
        rid, pid = topo.addr(dst)[:2]
        eng = topo.engines(core, dst)
        late = sum(moved(i) for o, i in moves)
        if len(moves) == 1:
            (out, in_), mask = moves[0], topo.mask(core, dst)
            return add("g", lambda: g.remote_dma(raw(out), raw(in_), T.sem[sem], T.sem.sent, pid, rid, mask), [in_], [], CALL,
                       "remote", len(eng), late)
        k = len(eng) // len(moves)
        masks = [sum(1 << e for e in eng[k * i:k * i + k]) for i in range(len(moves))]
        return add("g", lambda: g.remote_dma_fused(
            [RemoteDMATransfer(dst_ids=[DstId(rid=rid, pnc=pid)], dma_engine_mask=m, remote_sem=T.sem[sem], src=raw(i), dst=raw(o))
             for m, (o, i) in zip(masks, moves)], local_sem=T.sem.sent), [i for o, i in moves], [], CALL, "remote", len(eng), late)

    def arrive(src, outs, sem, calls):
        add("x", None, [], outs, 0.0, "ext", (sem, len(calls) * len(topo.engines(src, core)), calls))

    def spread(off):
        for q in (1, 2, 3):
            cp(quad(off, q), quad(off, 0))

    def spread2(off):
        cp(quad(off, 1), quad(off, 0))
        cp(half(off, 1), half(off, 0))

    def sspread(v):
        lin(quad(v, 1), quad(v, 0))
        lin(half(v, 1), half(v, 0))

    J, STAY, UNIQ, P32 = col("cc", 0), V("cc", 4, 6), col("cc", 6), col("cc", 10)
    PF, KF, QF = col("cc", 7), col("cc", 8), col("cc", 9)
    EDGE_L, EDGE_R = col("it", 84), col("it", 85)
    TRI, HALF, S4, J24 = V("tri", 0, 32), V("tri", 32, 64), V("s4", 0, 4), V("s4", 8, 32)
    WAYS = V("it", 72, 81)
    OE0, FIRST = V("ofs", 144, 150), V("ofs", 152, 164)
    plus = [("ew1", 0), ("ew2", 0), ("c", 144), ("c", 272)]
    minus = [("e", 128), ("ew0", 0), ("l", 0), ("f", 0)]
    own0 = me * A
    far0 = A - own0
    banks = [[("psd", 512 * b) for b in range(4)], [("pss", 0), ("pss", 512), ("psh", 0), ("psh", 512)]]

    def sm(t, i, n=1): return V("sm", 48 * t + i, 48 * t + i + n)
    def sd(k, t, i, n=1, step=1): return V(k, 16 * t + i, 16 * t + i + n, step)
    def of(t, i, n, step=1): return V("ofs", 48 * t + i, 48 * t + i + n, step)
    def gg(t, i, n, step=1): return V("gg", 64 * t + i, 64 * t + i + n, step)
    def osrv(t): return of(t, 0, 3)
    def oloc(t): return of(t, 4, 3)
    def oa(t): return of(t, 8, 3)
    def oslot(t): return of(t, 12, 12)
    def ox(t): return of(t, 24, 12)
    def oe(t): return of(t, 36, 6)
    def num(t): return V("nm", 8 * t + 1, 8 * t + 8, 2)
    def ed(t): return pair("ew%d" % t, 128, 224)
    def estat(t): return pair("ew%d" % t, 96, 224)
    def lstat(t): return pair("l", 96 + 96 * t, 224 + 96 * t)
    def slots(t): return pair("win%d" % t, 0, 192)
    def pf(buf, t, c0, c1): return V(buf, PW * t + c0, PW * t + c1)
    def note(t): return sd("sd1", t, 1, 3)
    def spot(t): return sd("sd1", t, 5)
    def low(t): return sd("sd1", t, 14)
    def key(t): return sd("so", t, 12)
    def zz(t): return sm(t, 35)

    def xs(t, b, k):
        c = 48 * b if k == 0 else 144 + 96 * b + 48 * k
        return V("xp%d" % t, c, c + 48)

    def best(ps, buf, stat, t, i, j0, out):
        lo, hi, ml, mh = pf(buf, t, 0, 512), pf(buf, t, 512, 1024), pf(buf, t, 511, 512), pf(buf, t, 1023, 1024)
        pb, cb = pf(buf, t, 1024, 1025), pf(buf, t, 1025, 1026)
        flip = t == 0 and me == 1
        for h in ((1, 0) if flip else (0, 1)):
            mm(V(ps, 512 * h, 512 * h + 512), stat, pair("h", 512 * h, 512 * h + 512))
        ja, jb = V("jk", j0, j0 + 512), V("jk", j0 + 512, j0 + 1024)
        if flip:
            scan(hi, V(ps, 512, 1024), V("zt", 0, 512), -BIG, alu.max, alu.add)
            count(jb, hi, mh, sm(t, i))
            ts(sm(t, i + 1), sm(t, i), 512.0, alu.add)
            scan(lo, V(ps, 0, 512), V("zt", 0, 512), -BIG, alu.max, alu.add)
            ts(sm(t, i + 2), ml, mh, alu.is_ge, -1.0, alu.mult)
            ts(sm(t, i + 3), ml, mh, alu.is_ge, ml, alu.mult)
            count(ja, lo, sm(t, i + 3), cb, sm(t, i + 2))
            ts(sm(t, i + 4), ml, mh, alu.is_lt, sm(t, i + 1), alu.mult)
            if out is None:
                ts(pb, sm(t, i + 4), shift, alu.add)
            else:
                ts(out, sm(t, i + 4), cb, alu.add)
            ts(mh, mh, ml, alu.max)
        elif out is None or t == 0:
            scan(lo, V(ps, 0, 512), V("zt", 0, 512), -BIG, alu.max, alu.add)
            count(ja, lo, ml, sm(t, i))
            scan(hi, V(ps, 512, 1024), V("zt", 0, 512), ml, alu.max, alu.add)
            count(jb, hi, mh, cb)
            ts(sm(t, i + 1), ml, mh, alu.is_lt, 512.0, alu.mult)
            if out is None:
                ts(pb, sm(t, i + 1), sm(t, i), alu.max, shift, alu.add)
            else:
                ts(out, sm(t, i + 1), sm(t, i), alu.max, cb, alu.add)
        else:
            scan(lo, V(ps, 0, 512), V("zt", 0, 512), -BIG, alu.max, alu.add)
            scan(hi, V(ps, 512, 1024), V("zt", 0, 512), ml, alu.max, alu.add)
            count(V("jk", j0, j0 + 1024), pf(buf, t, 0, 1024), mh, out)

    def send_e(t, land, src):
        calls = [send(peer, [(land[k], src[k])], "ae%d" % t) for k in (0, 1)]
        arrive(peer, list(land), "ae%d" % t, calls)

    def serve(t):
        best("pss", "psv", lstat(t), t, 36, 0, None)
        arrive(peer, [note(t)], "am%d" % t, [send(peer, [(note(t), pf("psv", t, 1023, 1026))], "am%d" % t)])
        for c in range(3):
            ts(quad(of(t, c, 1), 0), quad(pf("psv", t, 1024, 1025), c + 1), quad(pf("psv", t, 1025, 1026), c + 1), alu.add, -shift, alu.add)
        spread(osrv(t))
        c0 = 96 - 48 * t
        pick(pair("c", c0, c0 + 48), pair("h", 0, 1024), osrv(t))
        land = [V("win%dq" % t, 240, 288), V("win%ds" % t, 240, 432)]
        call = send(peer, [(land[0], V("cq", c0, c0 + 48)), (land[1], V("cs", c0, c0 + 192))], "ac%d" % t)
        arrive(peer, land, "ac%d" % t, [call])

    def worst(t):
        mm(V("psd", 1536, 1728), estat(t), slots(t))
        tt(V("ad", 0, 192), V("pen", 0, 192), V("psd", 1536, 1728), alu.subtract)
        scan(V("pa", 0, 192), V("ad", 0, 192), V("zt", 0, 192), -2 * BIG, alu.max, alu.add)
        count(V("jk", 2048, 2240), V("pa", 0, 192), col("pa", 191), low(t))

    def near(t):
        best("psh", "phm", estat(t), t, 41, 1024, spot(t))

    def near_picks(t):
        for c in range(3):
            cp(quad(of(t, 4 + c, 5, 4), 0), quad(sd("sd1", t, 5, 10, 9), c + 1))
        spread2(of(t, 4, 7))
        pick(pair("win%d" % t, 192, 240), pair("h", 0, 1024), oloc(t))
        pick(pair("f", 128 + 48 * t, 176 + 48 * t), slots(t), oa(t))
        ts(sm(t, 0, 4), num(t), spot(t), alu.is_equal, UNIQ, alu.mult)
        side(sm(t, 4), spot(t), EDGE_L)
        total(sd("sd1", t, 12), sm(t, 5, 5), sm(t, 0, 5), 1.0)
        total(sd("sd1", t, 11), sm(t, 10, 5), sm(t, 0, 5), -1.0)
        lin(sd("sd1", t, 4), spot(t), -1.0, 0.0, True)

    def move(t, k):
        end = 192 + 48 * k
        to = banks[k - 1]
        for b in range(4):
            mm(V(to[b][0], to[b][1], to[b][1] + 128), pair(minus[b][0], minus[b][1], minus[b][1] + 128), pair("f", 48 + 48 * t, 176 + 48 * t), True, False)
        for b in range(4):
            mm(V(to[b][0], to[b][1], to[b][1] + 128), pair(plus[b][0], plus[b][1], plus[b][1] + 128), pair("win%d" % t, end - 128, end), False, True)
        for b in range(4):
            tt(xs(t, b, k), V(to[b][0], to[b][1] + 80, to[b][1] + 128), xs(t, b, 0), alu.add)
        if t + 1 < R:
            for b in range(4):
                tt(V("et", 192 * (k - 1) + b, 192 * k, 4), V("bi", b, 192, 4), xs(t, b, k), alu.subtract)

    def y_out(t):
        for o in range(O):
            mm(V("psd", 512 * o, 512 * o + 192), pair("w", 128 * o, 128 * o + 128), slots(t + 1))
        for o in range(O):
            c = (t * O + o) * 192
            scopy(V("ys", c, c + 192), V("psd", 512 * o, 512 * o + 192))
        c = 576 * t
        if t + 1 < R:
            store("y", T.y[:, c:c + 576], V("ys", c, c + 576), [note(t + 1)])
        else:
            for o in range(O):
                store("y", T.y[:, c + 192 * o:c + 192 * o + 192], V("ys", c + 192 * o, c + 192 * o + 192))

    def decide(t):
        last = t + 1 == R
        mr, pb, cb, won = sd("sd1", t, 1), sd("sd1", t, 2), sd("sd1", t, 3), col("sd0", 5)
        ts(V("sd0", 5, 13, 7), V("zt", 0, 2), mr, alu.add, pf("phm", t, 1023, 1024), alu.is_gt if base_r > base_l else alu.is_ge)
        ts(sd("sd1", t, 6, 4), num(t), pb, alu.subtract, cb, alu.is_equal)
        either(lambda: side(sd("sd1", t, 10), pb, EDGE_R), lambda: ts(sd("sd1", t, 10), pb, A - 0.5 - shift, alu.is_gt, 1.0, alu.add))
        scan(sd("so", t, 2, 12), V("sd0", 2, 14), sd("sd1", t, 2, 12), 0.0, alu.mult, alu.add)
        scopy(quad(V("uu", 32, 64), 2), quad(HALF, 1), quad(key(t), 1))
        scopy(V("uu", 0, 32), TRI, key(t))
        scopy(quad(V("uu", 32, 64), 3), quad(HALF, 2), quad(key(t), 2))
        scopy(quad(V("uu", 64, 96), 3), quad(HALF, 1), quad(key(t), 1))
        tr(V("kk", 0, 96), V("uu", 0, 96))
        ts(V("sam", 0, 96), V("kk", 0, 96), key(t), alu.is_equal, -1000.0, alu.mult)
        red(zz(t), V("sam", 0, 97), alu.add)
        lin(sm(t, 33), won, 48.0, 0.0, True)
        lin(sm(t, 24, 9), WAYS, 1.0, sm(t, 33), True)
        ts(sm(t, 16, 4), S4, low(t), alu.is_equal, sd("so", t, 13), alu.mult)
        tt(sm(t, 20, 4), sm(t, 16, 4), sm(t, 29, 4), alu.min)
        if not last:
            for c in range(3):
                ts(quad(of(t, 36 + 2 * c, 2), 0), quad(STAY, c + 1), quad(zz(t), c + 1), alu.max, quad(sm(t, 28), c + 1), alu.min)
            spread(oe(t))
            quant("ew%d" % t, 224, 352, V("et", 0, 512))
            pick(ed(t + 1), pair("ew%d" % t, 128, 352), oe(t))
            send_e(t + 1, pair("l", 224 + 96 * t, 320 + 96 * t), ed(t + 1))
        for c in range(3):
            ts(quad(gg(t, c, 24 - c, 3), 0), quad(sm(t, 20, 8), c + 1), quad(zz(t), c + 1), alu.min, 0.0, alu.max)
        tt(quad(gg(t, 32, 24), 0), quad(gg(t, 0, 24), 0), quad(J24, 0), alu.add)
        both = of(t, 12, 24)
        for q in range(4 if last else 2):
            cp(quad(both, q), quad(gg(t, 32, 24), 0))
        if not last:
            cp(half(both, 1), half(both, 0))
        pick(slots(t + 1), pair("win%d" % t, 0, 288), oslot(t))
        if not last:
            gather(V("xp%d" % (t + 1), 0, 192), V("xp%d" % t, 0, 576), ox(t))
        else:
            for b in range(4):
                u = b % 2
                gather(V("pxs", 64 - 64 * u + b, 256, 4), V("xp%d" % t, 0, 576), of(t, 24 + 3 * b - u, 3 + u))
        lin(V("nm", 8 * t, 8 * t + 8, 2), num(t), -1.0, sd("so", t, 5), True)
        ts(V("rr", 1, 8, 2), sm(t, 20, 4), zz(t), alu.min, 0.0, alu.is_gt)
        scan(V("nm", 8 * t + 8, 8 * t + 16), V("rr", 0, 8), V("nm", 8 * t, 8 * t + 8), 0.0, alu.mult, alu.add)
        if last:
            for c in range(3):
                lin(quad(V("nt", c, 12, 3), 0), quad(num(R), c + 1), 1.0, quad(col("it", 86), c + 1), True)

    small = [load("y", V("xi", 0, 192), T.x[:, :]), load("s", V("bi", 0, 192), T.b[:, :])]
    first = load("y", V("di", 0, 4 * CUT), T.d[:, 0:4 * CUT], (), small)
    rest = load("s", V("di", 4 * CUT, 2048), T.d[:, 4 * CUT:2048], (), [first])
    load("y", V("ai", 0, 12, 1, 0, 16), T.act[:, :], (), [rest])
    load("s", V("ai", 0, 12, 1, 16, 32), T.act[:, :], (), [rest])
    iota(col("pi", 0), [[0, 1]], 1)
    iota(V("it", 0, 6), [[16, 3], [0, 2]])
    iota(V("it", 8, 40), [[0, 2], [1, 16]])
    iota(V("it", 40, 44), [[48, 4]], 0, -16)
    iota(V("it", 48, 72), [[0, 2], [16, 12]])
    iota(V("it", 72, 76), [[48, 4]], 0, 192)
    iota(V("it", 77, 81), [[-48, 4]], 0, 192)
    iota(V("it", 82, 84), [[0, 2]], 0, -32)
    iota(V("it", 84, 86), [[2 * int(shift), 2]], 0, 1 - 2 * A)
    iota(V("it", 86, 88), [[rank * A - 2 * base_l, 2]], 0, base_l)
    iota(V("sd0", 0, 16), [[0, 16]], 0, 1)
    iota(V("sd0", 2, 7, 4), [[0, 2]], 0, 0)
    iota(V("sd0", 11, 14, 2), [[-203, 2]], 0, 3)
    iota(V("sd1", 13, 48, 16), [[0, 3]], 0, 200 * CAPP)
    iota(col("sam", 96), [[0, 1]], 0, 1000 * CAPP - 500)
    iota(V("ip", 0, 192), [[0, 4], [1, 48]], 0, 16)
    iota(V("idn", 0, 128), [[-1, 128]], 1)
    ms(V("zt", 0, 576), 0.0)
    ms(V("ofs", 7, 144, 48), 0)
    lin(V("et", 192, 512), V("zt", 0, 320))
    ts(col("pi", 1), col("pi", 0), 15, alu.bitwise_and)
    ts(col("pi", 2), col("pi", 0), 1, alu.arith_shift_right, 48, alu.bitwise_and)
    cp(V("cc", 7, 10), V("pi", 0, 3))
    lin(P32, QF, -2.0, PF)
    ts(OE0, V("it", 0, 6), KF, alu.add)
    lin(J, KF, 1.0, QF)
    for i in range(2):
        lin(V("ct", 516 * i, 516 * i + 516), V("zt", 0, 516))
    ts(V("idn", 128, 256), V("idn", 0, 128), 0.0, alu.is_equal)
    for tiles, c in ((minus, -0.25), (plus, 0.25)):
        for i in range(2):
            lo = 516 * i + 2 + i
            lin(V("ct", lo, lo + 512, 4), V("idn", 128, 256), c)
        for b in range(4):
            lo = 516 * (b % 2) + 2 + b % 2 - b
            quant(tiles[b][0], tiles[b][1], tiles[b][1] + 128, V("ct", lo, lo + 512))
    tt(V("et", 0, 192), V("bi", 0, 192), V("xi", 0, 192), alu.subtract)
    lin(V("ad", 0, 192), V("ip", 0, 192), -1.0, J)
    add("s", lambda: g.scalar.activation(ap(V("pa", 0, 192)), ap(V("ad", 0, 192)), act.Abs), [V("ad", 0, 192)], [V("pa", 0, 192)], 192)
    lin(V("pen", 0, 192), V("pa", 0, 192), -BIG / 128)
    quant("e", 0, 128, V("et", 0, 512))
    land = [V("mq", 0, 48), V("ms", 0, 192)]
    arrive(peer, land, "ae0", [send(peer, [(land[0], V("eq", 0, 48)), (land[1], V("es", 0, 192))], "ae0")])
    pick(ed(0), pair("e", 0, 128), OE0)
    pick(pair("l", 128, 224), pair("m", 0, 48), OE0)
    for b in range(4):
        scopy(xs(0, b, 0), V("xi", b, 192, 4))
    quant("h", own0, own0 + CUT, V("di", 0, 4 * CUT))
    quant("h", own0 + CUT, own0 + A, V("di", 4 * CUT, 2048))
    v, u, s = V("hq", own0, own0 + CUT), V("hq", own0 + CUT, own0 + A), V("hs", own0, own0 + A)
    arrive(mate, [V("hq", far0, far0 + CUT)], "ah0", [send(mate, [(v, v)], "ah0")])
    arrive(mate, [V("hq", far0 + CUT, far0 + A), V("hs", far0, far0 + A)], "ah1", [send(mate, [(u, u), (s, s)], "ah1")])
    cp(quad(V("af", 0, 12), 0), quad(V("ai", 0, 12), 0))
    sspread(V("af", 0, 12))
    cp(FIRST, V("af", 0, 12))
    pick(slots(0), pair("h", own0, own0 + A), FIRST)
    lin(quad(num(0), 0), quad(V("zt", 0, 4), 0))
    for c in range(3):
        lin(quad(num(0), c + 1), quad(V("af", c, 12, 3), 0), 1.0, quad(col("it", 87), 0))
    lin(S4, V("it", 40, 44), 1.0, J)
    lin(J24, V("it", 48, 72), 1.0, KF)
    lin(UNIQ, J, 8.0)
    lin(col("cc", 1), J, 1.0, QF)
    lin(STAY, V("it", 82, 84), 1.0, col("cc", 1))
    lin(col("it", 76), col("s4", 2))
    ts(TRI, V("it", 8, 40), P32, alu.is_gt)
    ts(HALF, V("it", 8, 40), 15.5, alu.max, P32, alu.is_gt)
    lin(col("sd0", 10), UNIQ)
    lin(V("rr", 0, 8), V("zt", 0, 8))
    lin(V("uu", 32, 96), V("zt", 0, 64))
    lin(quad(V("nt", 12, 32), 0), quad(V("zt", 0, 20), 0))

    for t in range(R):
        if t == 0:
            worst(t)
        near(t)
        serve(t)
        if t == 0:
            load("y", V("wi", 0, 1536), T.w[:, :], [note(0)])
            for o in range(O):
                quant("w", 128 * o, 128 * o + 128, V("wi", 512 * o, 512 * o + 512))
        else:
            worst(t)
            y_out(t - 1)
        near_picks(t)
        move(t, 1)
        move(t, 2)
        decide(t)

    y_out(R - 1)
    store("y", T.oc[:, :], slots(R)[0])
    for k in range(4):
        store("ys"[k % 2], T.osc[4 * k:4 * k + 4, :], V("win%ds" % R, 0, 192, 1, 32 * k, 32 * k + 4))
    store("s", T.px[:, :], V("pxs", 64, 256))
    tr(quad(V("nt", 32, 64), 0), quad(V("nt", 0, 32), 0))
    store("y", T.an[:, :], V("nt", 32, 48, 1, 0, 12))
    emit(g, T, ops, me)
